import numpy as np
import ml_dtypes


def mxq(x, axis, fmt="e4m3"):
    dtype, down = {"e4m3": (ml_dtypes.float8_e4m3fn, 7), "e5m2": (ml_dtypes.float8_e5m2, 14)}[fmt]
    v = np.moveaxis(np.asarray(x, np.float32).astype(ml_dtypes.bfloat16).astype(np.float64), axis, -1)
    blocks = v.reshape(v.shape[:-1] + (-1, 32))
    amax = np.abs(blocks).max(-1, keepdims=True)
    byte = np.maximum(np.where(amax > 0, np.frexp(amax)[1] - 1 + 127, 0) - down, 1)
    scale = np.exp2(byte - 127.0)
    codes = (blocks / scale).astype(np.float32).astype(dtype).astype(np.float64)
    return np.moveaxis((codes * scale).reshape(v.shape), -1, axis)


WIDE = False


def mx_kscale(k):
    if not WIDE:
        return np.ones(k)
    levels = np.array([10, -10, 5, -5, 0])
    if k % 512:
        return np.exp2(np.random.permutation(np.resize(levels, k // 32))).repeat(32)
    a = np.empty((k // 512, 16))
    for p in range(k // 512):
        a[p, :8] = np.random.permutation(np.resize(levels, 8))
        for g in range(8):
            far = levels[np.abs(levels - a[p, g]) >= 10]
            a[p, g + 8] = far[np.random.randint(len(far))]
    return np.exp2(a.ravel()).repeat(32)


def f64(x):
    return np.asarray(x).astype(np.float64)


def striped(idx):
    return np.tile(idx.reshape(-1, 16).T, (8, 1)).astype(np.uint16)


def unstriped(offs):
    return offs[:16].T.reshape(-1).astype(np.int64)


E2M1 = np.array([0.0, 0.5, 1.0, 1.5, 2.0, 3.0, 4.0, 6.0, -0.0, -0.5, -1.0, -1.5, -2.0, -3.0, -4.0, -6.0])


def pack_weight(w, fmt):
    k, n = w.shape
    w = f64(np.asarray(w, np.float32).astype(ml_dtypes.bfloat16)).reshape(k // 32, 32, n)
    amax = np.abs(w).max(1)
    if fmt == "e4m3":
        byte = np.frexp(amax)[1] - 1 + 127 - 7
    else:
        mant, ex = np.frexp(amax / 6.0)
        byte = np.where(mant > 0.5, ex, ex - 1) + 127
    byte = np.clip(np.where(amax > 0, byte, 1), 1, 254)
    scaled = (w * np.exp2(127.0 - byte)[:, None, :]).reshape(k, n).astype(np.float32)
    by_word = np.ascontiguousarray(scaled.reshape(k // 512, 128, 4, n).transpose(0, 1, 3, 2))
    if fmt == "e4m3":
        words = by_word.astype(ml_dtypes.float8_e4m3fn).view(np.uint8)
    else:
        c = by_word.astype(ml_dtypes.float4_e2m1fn).view(np.uint8) & 0xF
        words = (c[..., 0::2] | (c[..., 1::2] << 4)).reshape(k // 512, 128, 2 * n)
    return np.ascontiguousarray(words), np.ascontiguousarray(byte.astype(np.uint8).reshape(k // 512, 16, n))


def unpack_weight(words, scales, fmt):
    g, _, n = scales.shape
    words = np.ascontiguousarray(words).reshape(g, 128, n, -1)
    if fmt == "e4m3":
        vals = words.view(ml_dtypes.float8_e4m3fn).astype(np.float64)
    else:
        nib = np.empty((g, 128, n, 4), np.uint8)
        nib[..., 0::2] = words & 0xF
        nib[..., 1::2] = words >> 4
        vals = E2M1[nib]
    vals = vals * np.repeat(np.exp2(scales.astype(np.float64) - 127.0), 8, axis=1)[..., None]
    return vals.transpose(0, 1, 3, 2).reshape(g * 512, n)


K, T, E, C, N = 256, 1024, 8, 256, 512


def by_expert(wq, xq):
    return np.concatenate([wq[e].T @ xq[:, e * C:(e + 1) * C] for e in range(E)], axis=1)


def setup_inputs():
    n = np.random.standard_normal
    v = mx_kscale(N)
    first = np.random.permutation(np.repeat(np.arange(E), T // E))
    second = (first + 1 + np.random.permutation(np.repeat(np.arange(E - 1), -(-T // (E - 1)))[:T])) % E
    while np.bincount(second, minlength=E).max() != T // E:
        load = np.bincount(second, minlength=E); hi, lo = int(load.argmax()), int(load.argmin())
        t = np.flatnonzero((second == hi) & (first != lo))[0]; second[t] = lo
    slot_token = np.empty(E * C, np.int64); pos = np.empty((2, T), np.int64); fill = np.zeros(E, np.int64)
    place = np.stack([np.random.permutation(C) for _ in range(E)])
    for r, deal in enumerate((first, second)):
        for t in np.random.permutation(T):
            e = deal[t]; j = e * C + place[e, fill[e]]; fill[e] += 1; slot_token[j] = t; pos[r, t] = j
    g = np.random.uniform(0.2, 0.8, T)
    w_slot = np.empty(E * C); w_slot[pos[0]] = g; w_slot[pos[1]] = 1.0 - g
    dq = pack_weight(n((N, T)) * v[:, None], "e4m3")
    dk = pack_weight(n((N, T)) * v[:, None], "e4m3")
    dv = pack_weight(n((N, T)) * v[:, None], "e4m3")
    wq = [pack_weight(m, "e4m3") for m in n((E, N, K)) / np.sqrt(N) / v[None, :, None]]
    wv = [pack_weight(m, "e4m3") for m in n((E, N, K)) / np.sqrt(N) / v[None, :, None]]
    return {
        "dq_words": dq[0],
        "dq_scales": dq[1],
        "dk_words": dk[0],
        "dk_scales": dk[1],
        "dv_words": dv[0],
        "dv_scales": dv[1],
        "wq_words": np.stack([m[0] for m in wq]),
        "wq_scales": np.stack([m[1] for m in wq]),
        "wk": (n((E, N, K)) / np.sqrt(N) / v[None, :, None]).astype(np.float32),
        "wv_words": np.stack([m[0] for m in wv]),
        "wv_scales": np.stack([m[1] for m in wv]),
        "gate": (np.tile(w_slot, (128, 1))).astype(np.float32),
        "offs": striped(slot_token),
        "pos1": striped(pos[0]),
        "pos2": striped(pos[1]),
    }


def reference(dq_words, dq_scales, dk_words, dk_scales, dv_words, dv_scales, wq_words, wq_scales, wk, wv_words, wv_scales, gate, offs, pos1, pos2):
    wq = np.stack([unpack_weight(wq_words[e], wq_scales[e], "e4m3") for e in range(E)])
    wkq = mxq(f64(wk), 1, "e4m3")
    wv = np.stack([unpack_weight(wv_words[e], wv_scales[e], "e4m3") for e in range(E)])
    idx = unstriped(offs)
    gq, gk, gv = [unpack_weight(w, s, "e4m3")[:, idx] for w, s in ((dq_words, dq_scales), (dk_words, dk_scales), (dv_words, dv_scales))]
    dx = f64(gate[:1]) * (by_expert(wq, gq) + by_expert(wkq, gk) + by_expert(wv, gv))
    out = dx[:, unstriped(pos1)] + dx[:, unstriped(pos2)]
    return out

@@ -1,0 +1,232 @@
+from contextlib import ExitStack
+
+import concourse.mybir as mybir
+from concourse.masks import make_identity
+
+K, T, E, C, N = 256, 1024, 8, 256, 512
+FLOPS = 2 * 3 * N * K * E * C
+
+F32 = mybir.dt.float32
+BF16 = mybir.dt.bfloat16
+I32 = mybir.dt.int32
+U32 = mybir.dt.uint32
+U16 = mybir.dt.uint16
+U8 = mybir.dt.uint8
+FP8X4 = mybir.dt.float8_e4m3fn_x4
+COPY = mybir.ActivationFunctionType.Copy
+MULT = mybir.AluOpType.mult
+ADD = mybir.AluOpType.add
+
+P = 128
+S = E * C
+PAIR = 2 * C
+PAIRS = E // 2
+TURNED = E - 2
+LIST = 16
+
+
+def tile_moe_qkb_kernel(
+    tc, dq_words, dq_scales, dk_words, dk_scales, dv_words, dv_scales,
+    wq_words, wq_scales, wk, wv_words, wv_scales, gate, offs, pos1, pos2, out,
+):
+    nc = tc.nc
+    with ExitStack() as ctx:
+        keep = ctx.enter_context(tc.tile_pool(name="keep", bufs=1))
+        share = ctx.enter_context(tc.tile_pool(name="share", bufs=1))
+        ring = ctx.enter_context(tc.tile_pool(name="ring", bufs=3))
+        psum = ctx.enter_context(tc.psum_pool(name="psum", bufs=1))
+
+        offs_sb = keep.tile([P, S // LIST], U16, name="offs_sb")
+        pos1_sb = keep.tile([P, T // LIST], U16, name="pos1_sb")
+        pos2_sb = keep.tile([P, T // LIST], U16, name="pos2_sb")
+        names = ("q", "k", "v")
+        d_words = [keep.tile([P, T], I32, name=f"d{n}_words_sb", align_bytes=64) for n in names]
+        d_scales = [keep.tile([P, T], U8, name=f"d{n}_scales_sb", align_bytes=64) for n in names]
+        w_scales = {n: keep.tile([P, E, K], U8, name=f"w{n}_scales_sb", align_bytes=64) for n in ("q", "v")}
+        w_words = {(n, h): keep.tile([P, E // 2, K], I32, name=f"w{n}_words_sb{h}", align_bytes=64)
+                   for n in ("q", "v") for h in range(2)}
+        wk_raw = [keep.tile([P, 4, K], F32, name=f"wk_raw{e}") for e in range(E)]
+        gate_rows = keep.tile([P, P], F32, name="gate_rows")
+        gate_cols = keep.tile([P, S // P], F32, name="gate_cols")
+        gate_last = keep.tile([P, S - TURNED * C], F32, name="gate_last")
+        identity = keep.tile([P, P], F32, name="identity")
+        dx = [keep.tile([P, S], F32, name=f"dx{cb}") for cb in range(2)]
+
+        for plane in d_scales:
+            nc.vector.memset(plane[:].bitcast(I32), 0)
+        for plane in w_scales.values():
+            nc.gpsimd.memset(plane[:].rearrange("p e c -> p (e c)").bitcast(I32), 0)
+        nc.gpsimd.memset(gate_rows[:], 0.0)
+        make_identity(nc, identity[:])
+
+        def load_words(i, src):
+            nc.sync.dma_start(d_words[i][:], src[0].rearrange("p t d -> p (t d)").bitcast(I32))
+
+        def load_scales(i, src):
+            for r in range(4):
+                nc.sync.dma_start(d_scales[i][r:P:32, :].bitcast(I32), src[0].bitcast(I32)[r:16:4, :])
+
+        def load_w_scales(n, src):
+            rows = src.rearrange("e s b c -> (s b) e c").bitcast(I32)
+            for r in range(4):
+                nc.sync.dma_start(w_scales[n][r:P:32, :, :].bitcast(I32), rows[r:16:4, :, :])
+
+        def load_w_words(n, h, src):
+            half = src[4 * h: 4 * h + 4].rearrange("e s p c d -> p (e s) (c d)").bitcast(I32)
+            nc.sync.dma_start(w_words[n, h][:], half)
+
+        def load_wk(e):
+            nc.sync.dma_start(wk_raw[e][:], wk[e].rearrange("(p j) c -> p j c", j=4))
+
+        nc.sync.dma_start(offs_sb[:], offs)
+        load_words(0, dq_words)
+        load_words(1, dk_words)
+        load_words(2, dv_words)
+        load_scales(0, dq_scales)
+        load_wk(0)
+        load_scales(1, dk_scales)
+        load_wk(1)
+        load_scales(2, dv_scales)
+        load_wk(2)
+        load_wk(3)
+        nc.sync.dma_start(gate_rows[0:S // P, :], gate[0].rearrange("(b p) -> b p", p=P))
+        load_w_words("q", 0, wq_words)
+        load_w_scales("q", wq_scales)
+        load_w_words("v", 0, wv_words)
+        load_w_scales("v", wv_scales)
+        for e in range(4, E):
+            load_wk(e)
+        load_w_words("q", 1, wq_words)
+        load_w_words("v", 1, wv_words)
+        nc.sync.dma_start(gate_last[:], gate[:, TURNED * C:])
+        nc.sync.dma_start(pos1_sb[:], pos1)
+        nc.sync.dma_start(pos2_sb[:], pos2)
+
+        gate_bank = psum.tile([P, P], F32, name="gate_bank", tag="turn00")
+        nc.tensor.transpose(gate_bank[:], gate_rows[:], identity[:])
+        nc.scalar.copy(gate_cols[:], gate_bank[:, 0:S // P])
+
+        REGION = 8192
+        g_words, g_scales = {}, {}
+
+        def gathered_tiles(pair):
+            if pair < 2:
+                for i, n in enumerate(names):
+                    g_words[pair, i] = keep.tile([P, PAIR], U32, name=f"g{n}w{pair}", align_bytes=64)
+                    g_scales[pair, i] = keep.tile([P, PAIR], U8, name=f"g{n}s{pair}", align_bytes=64)
+            else:
+                base = (pair - 2) * REGION
+                for i, n in enumerate(names):
+                    g_words[pair, i] = share.tile([P, PAIR], U32, name=f"g{n}w{pair}", align_bytes=64,
+                                                  offset=base + (64, 3648, 5696)[i])
+                    g_scales[pair, i] = share.tile([P, PAIR], U8, name=f"g{n}s{pair}", align_bytes=64,
+                                                   offset=base + 2112 + 512 * i)
+
+        def gather(pair, i, lo, hi, words):
+            entries = offs_sb[:, (pair * PAIR + lo) // LIST:(pair * PAIR + hi) // LIST]
+            if words:
+                nc.vector.tensor_copy(g_words[pair, i][:, lo:hi], d_words[i][:].bitcast(U32).indirect(entries))
+            else:
+                nc.vector.tensor_copy(g_scales[pair, i][:, lo:hi], d_scales[i][:].indirect(entries))
+
+        wk_codes, wk_scales = {}, {}
+
+        def quantise_pair(pair):
+            if pair % 2:
+                cast = share.tile([P, 2, K, 4], BF16, name=f"cast{pair}", align_bytes=64,
+                                  offset=(pair // 2) * REGION + 2048)
+            else:
+                cast = keep.tile([P, 2, K, 4], BF16, name=f"cast{pair}", align_bytes=64)
+            for j in range(2):
+                nc.scalar.copy(cast[:, j].rearrange("p (c i) t -> p c t i", i=4),
+                               wk_raw[2 * pair + j][:].rearrange("p t (c i) -> p c t i", i=4))
+            wk_codes[pair] = keep.tile([P, 2, K], U32, name=f"wk_codes{pair}", align_bytes=64)
+            wk_scales[pair] = keep.tile([P, 2, K], U8, name=f"wk_scales{pair}", align_bytes=64)
+            nc.vector.quantize_mx(out=wk_codes[pair][:].rearrange("p j c -> p (j c)").bitcast(FP8X4),
+                                  scales=wk_scales[pair][:].rearrange("p j c -> p (j c)"),
+                                  in_=cast[:].rearrange("p j c t -> p (j c t)"))
+
+        def weights(e, i, cols):
+            if i == 1:
+                return wk_codes[e // 2][:, e % 2, cols].bitcast(FP8X4), wk_scales[e // 2][:, e % 2, cols]
+            n = names[i]
+            return w_words[n, e // 4][:, e % 4, cols].bitcast(FP8X4), w_scales[n][:, e, cols]
+
+        def grads(e, i, lo, hi):
+            cols = slice((e % 2) * C + lo, (e % 2) * C + hi)
+            return g_words[e // 2, i][:, cols].bitcast(FP8X4), g_scales[e // 2, i][:, cols]
+
+        def turned_expert(e):
+            sums = psum.tile([P, 2, K], F32, name=f"sums{e}", tag=f"sums{e % 2}")
+            for blk in range(2):
+                for i in range(3):
+                    gw, gs = grads(e, i, blk * P, (blk + 1) * P)
+                    ww, ws = weights(e, i, slice(0, K))
+                    nc.tensor.matmul_mx(out=sums[:, blk, :], lhsT=gw, lhsT_scale=gs, rhs=ww, rhs_scale=ws,
+                                        start=(i == 0), stop=(i == 2))
+            gated = ring.tile([P, 2, K], F32, name="gated")
+            for blk in range(2):
+                b = 2 * e + blk
+                nc.scalar.activation(gated[:, blk, :], sums[:, blk, :], COPY, scale=gate_cols[:, b:b + 1])
+            turns = [psum.tile([P, C], F32, name=f"turn{e}_{cb}", tag=f"turn{e % 2}{cb}") for cb in range(2)]
+            for blk in range(2):
+                for cb in range(2):
+                    nc.tensor.transpose(turns[cb][:, blk * P:(blk + 1) * P], gated[:, blk, cb * P:(cb + 1) * P], identity[:])
+            for cb in range(2):
+                nc.scalar.copy(dx[cb][:, e * C:(e + 1) * C], turns[cb][:])
+
+        def direct_pass(e, i, cb, bank):
+            gw, gs = grads(e, i, 0, C)
+            ww, ws = weights(e, i, slice(cb * P, (cb + 1) * P))
+            nc.tensor.matmul_mx(out=bank, lhsT=ww, lhsT_scale=ws, rhs=gw, rhs_scale=gs,
+                                start=(i == 0), stop=(i == 2))
+
+        def direct_gate(e, cb, bank):
+            nc.vector.tensor_tensor(dx[cb][:, e * C:(e + 1) * C], bank,
+                                    gate_last[:, (e - TURNED) * C:(e - TURNED + 1) * C], MULT)
+
+        gathered_tiles(0)
+        gathered_tiles(1)
+        for words in (True, False):
+            for i in range(3):
+                for pair in range(2):
+                    gather(pair, i, 0, PAIR, words)
+        quantise_pair(0)
+        quantise_pair(1)
+        gathered_tiles(2)
+        for i in range(3):
+            for words in (True, False):
+                gather(2, i, 0, PAIR, words)
+        for e in range(4):
+            turned_expert(e)
+        quantise_pair(2)
+        quantise_pair(3)
+        gathered_tiles(3)
+        for j in range(2):
+            for i in range(3):
+                for words in (True, False):
+                    gather(3, i, j * C, (j + 1) * C, words)
+        turned_expert(4)
+        turned_expert(5)
+
+        sums6 = psum.tile([P, 2, C], F32, name="sums6", tag="sums1")
+        for cb in range(2):
+            for i in range(3):
+                direct_pass(6, i, cb, sums6[:, cb, :])
+        sums7 = [psum.tile([P, C], F32, name=f"sums7_{cb}", tag=f"turn1{cb}") for cb in range(2)]
+        for i in range(3):
+            for cb in range(2):
+                direct_pass(7, i, cb, sums7[cb][:])
+        for cb in range(2):
+            direct_gate(6, cb, sums6[:, cb, :])
+        for cb in range(2):
+            direct_gate(7, cb, sums7[cb][:])
+
+        firsts = [keep.tile([P, T], F32, name=f"first{cb}") for cb in range(2)]
+        for cb in range(2):
+            nc.vector.tensor_copy(firsts[cb][:], dx[cb][:].indirect(pos1_sb[:]))
+        for cb, lo, hi in ((0, 0, T), (1, 0, 768), (1, 768, T)):
+            both = keep.tile([P, hi - lo], F32, name=f"both{cb}_{lo}")
+            nc.vector.tensor_tensor(both[:], dx[cb][:].indirect(pos2_sb[:, lo // LIST:hi // LIST]),
+                                    firsts[cb][:, lo:hi], ADD)
+            nc.sync.dma_start(out[cb * P:(cb + 1) * P, lo:hi], both[:])

@@ -23,6 +23,7 @@ PAIR = 2 * C
 PAIRS = E // 2
 TURNED = E - 2
 LIST = 16
+WIDE = 1376
 
 
 def tile_moe_qkb_kernel(
@@ -33,38 +34,38 @@ def tile_moe_qkb_kernel(
     with ExitStack() as ctx:
         keep = ctx.enter_context(tc.tile_pool(name="keep", bufs=1))
         share = ctx.enter_context(tc.tile_pool(name="share", bufs=1))
-        ring = ctx.enter_context(tc.tile_pool(name="ring", bufs=3))
         psum = ctx.enter_context(tc.psum_pool(name="psum", bufs=1))
 
         offs_sb = keep.tile([P, S // LIST], U16, name="offs_sb")
         pos1_sb = keep.tile([P, T // LIST], U16, name="pos1_sb")
         pos2_sb = keep.tile([P, T // LIST], U16, name="pos2_sb")
         names = ("q", "k", "v")
-        d_words = [keep.tile([P, T], I32, name=f"d{n}_words_sb", align_bytes=64) for n in names]
-        d_scales = [keep.tile([P, T], U8, name=f"d{n}_scales_sb", align_bytes=64) for n in names]
+        d_words = [keep.tile([P, WIDE], I32, name=f"d{n}_words_sb", align_bytes=64) for n in names]
+        d_scales = [keep.tile([P, WIDE], U8, name=f"d{n}_scales_sb", align_bytes=64) for n in names]
         w_scales = {n: keep.tile([P, E, K], U8, name=f"w{n}_scales_sb", align_bytes=64) for n in ("q", "v")}
         w_words = {(n, h): keep.tile([P, E // 2, K], I32, name=f"w{n}_words_sb{h}", align_bytes=64)
                    for n in ("q", "v") for h in range(2)}
-        wk_raw = [keep.tile([P, 4, K], F32, name=f"wk_raw{e}") for e in range(E)]
+        wk_raw = [keep.tile([P, 4, K], F32, name=f"wk_raw{e}", tag=f"raw{e}") for e in range(E)]
         gate_rows = keep.tile([P, P], F32, name="gate_rows")
         gate_cols = keep.tile([P, S // P], F32, name="gate_cols")
         gate_last = keep.tile([P, S - TURNED * C], F32, name="gate_last")
         identity = keep.tile([P, P], F32, name="identity")
         dx = [keep.tile([P, S], F32, name=f"dx{cb}") for cb in range(2)]
 
+        nc.vector.memset(d_words[0][:, T:], 0)
         for plane in d_scales:
             nc.vector.memset(plane[:].bitcast(I32), 0)
-        for plane in w_scales.values():
-            nc.gpsimd.memset(plane[:].rearrange("p e c -> p (e c)").bitcast(I32), 0)
+        for table in d_words[1:]:
+            nc.vector.memset(table[:, T:], 0)
         nc.gpsimd.memset(gate_rows[:], 0.0)
         make_identity(nc, identity[:])
 
         def load_words(i, src):
-            nc.sync.dma_start(d_words[i][:], src[0].rearrange("p t d -> p (t d)").bitcast(I32))
+            nc.sync.dma_start(d_words[i][:, :T], src[0].rearrange("p t d -> p (t d)").bitcast(I32))
 
         def load_scales(i, src):
             for r in range(4):
-                nc.sync.dma_start(d_scales[i][r:P:32, :].bitcast(I32), src[0].bitcast(I32)[r:16:4, :])
+                nc.sync.dma_start(d_scales[i][r:P:32, :T].bitcast(I32), src[0].bitcast(I32)[r:16:4, :])
 
         def load_w_scales(n, src):
             rows = src.rearrange("e s b c -> (s b) e c").bitcast(I32)
@@ -87,15 +88,13 @@ def tile_moe_qkb_kernel(
         load_scales(1, dk_scales)
         load_wk(1)
         load_scales(2, dv_scales)
-        load_wk(2)
-        load_wk(3)
+        for e in range(2, E):
+            load_wk(e)
         nc.sync.dma_start(gate_rows[0:S // P, :], gate[0].rearrange("(b p) -> b p", p=P))
         load_w_words("q", 0, wq_words)
         load_w_scales("q", wq_scales)
         load_w_words("v", 0, wv_words)
         load_w_scales("v", wv_scales)
-        for e in range(4, E):
-            load_wk(e)
         load_w_words("q", 1, wq_words)
         load_w_words("v", 1, wv_words)
         nc.sync.dma_start(gate_last[:], gate[:, TURNED * C:])
@@ -107,126 +106,126 @@ def tile_moe_qkb_kernel(
         nc.scalar.copy(gate_cols[:], gate_bank[:, 0:S // P])
 
         REGION = 8192
+        CHUNKS = ((0, 4), (4, 6), (6, 8))
         g_words, g_scales = {}, {}
 
-        def gathered_tiles(pair):
-            if pair < 2:
-                for i, n in enumerate(names):
-                    g_words[pair, i] = keep.tile([P, PAIR], U32, name=f"g{n}w{pair}", align_bytes=64)
-                    g_scales[pair, i] = keep.tile([P, PAIR], U8, name=f"g{n}s{pair}", align_bytes=64)
-            else:
-                base = (pair - 2) * REGION
-                for i, n in enumerate(names):
-                    g_words[pair, i] = share.tile([P, PAIR], U32, name=f"g{n}w{pair}", align_bytes=64,
-                                                  offset=base + (64, 3648, 5696)[i])
-                    g_scales[pair, i] = share.tile([P, PAIR], U8, name=f"g{n}s{pair}", align_bytes=64,
-                                                   offset=base + 2112 + 512 * i)
+        def gathered_tiles(ch):
+            width = (CHUNKS[ch][1] - CHUNKS[ch][0]) * C
+            for i, n in enumerate(names):
+                if ch == 0:
+                    g_words[ch, i] = keep.tile([P, width], U32, name=f"g{n}w{ch}", align_bytes=64)
+                    g_scales[ch, i] = keep.tile([P, width], U8, name=f"g{n}s{ch}", align_bytes=64)
+                else:
+                    base = (ch - 1) * REGION + i * 5 * width
+                    g_words[ch, i] = share.tile([P, width], U32, name=f"g{n}w{ch}", align_bytes=64, offset=base)
+                    g_scales[ch, i] = share.tile([P, width], U8, name=f"g{n}s{ch}", align_bytes=64,
+                                                 offset=base + 4 * width)
 
-        def gather(pair, i, lo, hi, words):
-            entries = offs_sb[:, (pair * PAIR + lo) // LIST:(pair * PAIR + hi) // LIST]
-            if words:
-                nc.vector.tensor_copy(g_words[pair, i][:, lo:hi], d_words[i][:].bitcast(U32).indirect(entries))
-            else:
-                nc.vector.tensor_copy(g_scales[pair, i][:, lo:hi], d_scales[i][:].indirect(entries))
+        def entries(ch, lo, hi):
+            first = CHUNKS[ch][0] * C
+            return offs_sb[:, (first + lo) // LIST:(first + hi) // LIST]
 
-        wk_codes, wk_scales = {}, {}
+        def gather_words(ch, i, lo, hi):
+            nc.vector.tensor_copy(g_words[ch, i][:, lo:hi], d_words[i][:].bitcast(U32).indirect(entries(ch, lo, hi)))
 
-        def quantise_pair(pair):
-            if pair % 2:
-                cast = share.tile([P, 2, K, 4], BF16, name=f"cast{pair}", align_bytes=64,
-                                  offset=(pair // 2) * REGION + 2048)
-            else:
-                cast = keep.tile([P, 2, K, 4], BF16, name=f"cast{pair}", align_bytes=64)
-            for j in range(2):
-                nc.scalar.copy(cast[:, j].rearrange("p (c i) t -> p c t i", i=4),
-                               wk_raw[2 * pair + j][:].rearrange("p t (c i) -> p c t i", i=4))
-            wk_codes[pair] = keep.tile([P, 2, K], U32, name=f"wk_codes{pair}", align_bytes=64)
-            wk_scales[pair] = keep.tile([P, 2, K], U8, name=f"wk_scales{pair}", align_bytes=64)
-            nc.vector.quantize_mx(out=wk_codes[pair][:].rearrange("p j c -> p (j c)").bitcast(FP8X4),
-                                  scales=wk_scales[pair][:].rearrange("p j c -> p (j c)"),
-                                  in_=cast[:].rearrange("p j c t -> p (j c t)"))
+        def gather_scales(ch, i, lo, hi):
+            nc.vector.tensor_copy(g_scales[ch, i][:, lo:hi], d_scales[i][:].indirect(entries(ch, lo, hi)))
+
+        def gather(ch, i, lo, hi):
+            gather_words(ch, i, lo, hi)
+            gather_scales(ch, i, lo, hi)
+
+        wk_codes, wk_scales, casts = {}, {}, {}
+
+        def cast_half(h):
+            cast = share.tile([P, 4, K, 4], BF16, name=f"cast{h}", align_bytes=64, offset=h * REGION)
+            for j in range(4):
+                nc.scalar.copy(cast[:, j], wk_raw[4 * h + j][:].rearrange("p t c -> p c t"))
+            casts[h] = cast
+
+        def quantise_half(h):
+            wk_codes[h] = keep.tile([P, 4, K], U32, name=f"wk_codes{h}", align_bytes=64)
+            wk_scales[h] = keep.tile([P, 4, K], U8, name=f"wk_scales{h}", align_bytes=64)
+            nc.vector.quantize_mx(out=wk_codes[h][:].rearrange("p j c -> p (j c)").bitcast(FP8X4),
+                                  scales=wk_scales[h][:].rearrange("p j c -> p (j c)"),
+                                  in_=casts[h][:].rearrange("p j c t -> p (j c t)"))
 
         def weights(e, i, cols):
             if i == 1:
-                return wk_codes[e // 2][:, e % 2, cols].bitcast(FP8X4), wk_scales[e // 2][:, e % 2, cols]
+                return wk_codes[e // 4][:, e % 4, cols].bitcast(FP8X4), wk_scales[e // 4][:, e % 4, cols]
             n = names[i]
             return w_words[n, e // 4][:, e % 4, cols].bitcast(FP8X4), w_scales[n][:, e, cols]
 
         def grads(e, i, lo, hi):
-            cols = slice((e % 2) * C + lo, (e % 2) * C + hi)
-            return g_words[e // 2, i][:, cols].bitcast(FP8X4), g_scales[e // 2, i][:, cols]
+            ch = max(0, e // 2 - 1)
+            first = (e - CHUNKS[ch][0]) * C
+            cols = slice(first + lo, first + hi)
+            return g_words[ch, i][:, cols].bitcast(FP8X4), g_scales[ch, i][:, cols]
 
-        def turned_expert(e):
-            sums = psum.tile([P, 2, K], F32, name=f"sums{e}", tag=f"sums{e % 2}")
+        def turned(e, cbs, sums_tag, turn_tags):
+            cols = slice(cbs[0] * P, (cbs[-1] + 1) * P)
+            width = len(cbs) * P
+            sums = psum.tile([P, 2, width], F32, name=f"sums{e}", tag=sums_tag)
             for blk in range(2):
                 for i in range(3):
                     gw, gs = grads(e, i, blk * P, (blk + 1) * P)
-                    ww, ws = weights(e, i, slice(0, K))
+                    ww, ws = weights(e, i, cols)
                     nc.tensor.matmul_mx(out=sums[:, blk, :], lhsT=gw, lhsT_scale=gs, rhs=ww, rhs_scale=ws,
                                         start=(i == 0), stop=(i == 2))
-            gated = ring.tile([P, 2, K], F32, name="gated")
+            gated = keep.tile([P, 2, width], F32, name=f"gated{e}", tag=f"raw{E - 1 - e % 3}")
             for blk in range(2):
                 b = 2 * e + blk
                 nc.scalar.activation(gated[:, blk, :], sums[:, blk, :], COPY, scale=gate_cols[:, b:b + 1])
-            turns = [psum.tile([P, C], F32, name=f"turn{e}_{cb}", tag=f"turn{e % 2}{cb}") for cb in range(2)]
+            turns = [psum.tile([P, C], F32, name=f"turn{e}_{cb}", tag=tag) for cb, tag in zip(cbs, turn_tags)]
             for blk in range(2):
-                for cb in range(2):
-                    nc.tensor.transpose(turns[cb][:, blk * P:(blk + 1) * P], gated[:, blk, cb * P:(cb + 1) * P], identity[:])
-            for cb in range(2):
-                nc.scalar.copy(dx[cb][:, e * C:(e + 1) * C], turns[cb][:])
+                for j in range(len(cbs)):
+                    nc.tensor.transpose(turns[j][:, blk * P:(blk + 1) * P], gated[:, blk, j * P:(j + 1) * P], identity[:])
+            for j, cb in enumerate(cbs):
+                nc.scalar.copy(dx[cb][:, e * C:(e + 1) * C], turns[j][:])
 
-        def direct_pass(e, i, cb, bank):
-            gw, gs = grads(e, i, 0, C)
-            ww, ws = weights(e, i, slice(cb * P, (cb + 1) * P))
-            nc.tensor.matmul_mx(out=bank, lhsT=ww, lhsT_scale=ws, rhs=gw, rhs_scale=gs,
-                                start=(i == 0), stop=(i == 2))
-
-        def direct_gate(e, cb, bank):
-            nc.vector.tensor_tensor(dx[cb][:, e * C:(e + 1) * C], bank,
+        def direct_sums(e, tag):
+            sums = psum.tile([P, C], F32, name=f"direct{e}", tag=tag)
+            for i in range(3):
+                gw, gs = grads(e, i, 0, C)
+                ww, ws = weights(e, i, slice(0, P))
+                nc.tensor.matmul_mx(out=sums[:], lhsT=ww, lhsT_scale=ws, rhs=gw, rhs_scale=gs,
+                                    start=(i == 0), stop=(i == 2))
+            nc.vector.tensor_tensor(dx[0][:, e * C:(e + 1) * C], sums[:],
                                     gate_last[:, (e - TURNED) * C:(e - TURNED + 1) * C], MULT)
 
+        cast_half(0)
+        cast_half(1)
         gathered_tiles(0)
+        for i in range(3):
+            gather_words(0, i, 0, 4 * C)
+        for i in range(3):
+            gather_scales(0, i, 0, 4 * C)
+        quantise_half(0)
         gathered_tiles(1)
-        for words in (True, False):
-            for i in range(3):
-                for pair in range(2):
-                    gather(pair, i, 0, PAIR, words)
-        quantise_pair(0)
-        quantise_pair(1)
-        gathered_tiles(2)
         for i in range(3):
-            for words in (True, False):
-                gather(2, i, 0, PAIR, words)
+            gather(1, i, 0, PAIR)
         for e in range(4):
-            turned_expert(e)
-        quantise_pair(2)
-        quantise_pair(3)
-        gathered_tiles(3)
+            turned(e, (0, 1), f"sums{e % 2}", (f"turn{e % 2}0", f"turn{e % 2}1"))
+        quantise_half(1)
+        gathered_tiles(2)
+        for i in range(2):
+            gather(2, i, 0, PAIR)
         for j in range(2):
-            for i in range(3):
-                for words in (True, False):
-                    gather(3, i, j * C, (j + 1) * C, words)
-        turned_expert(4)
-        turned_expert(5)
+            gather(2, 2, j * C, (j + 1) * C)
+        for e in (4, 5):
+            turned(e, (0, 1), f"sums{e % 2}", (f"turn{e % 2}0", f"turn{e % 2}1"))
+        direct_sums(6, "sums1")
+        direct_sums(7, "turn11")
+        turned(6, (1,), "turn10", ("turn00",))
+        turned(7, (1,), "turn10", ("turn01",))
 
-        sums6 = psum.tile([P, 2, C], F32, name="sums6", tag="sums1")
         for cb in range(2):
-            for i in range(3):
-                direct_pass(6, i, cb, sums6[:, cb, :])
-        sums7 = [psum.tile([P, C], F32, name=f"sums7_{cb}", tag=f"turn1{cb}") for cb in range(2)]
-        for i in range(3):
-            for cb in range(2):
-                direct_pass(7, i, cb, sums7[cb][:])
-        for cb in range(2):
-            direct_gate(6, cb, sums6[:, cb, :])
-        for cb in range(2):
-            direct_gate(7, cb, sums7[cb][:])
-
-        firsts = [keep.tile([P, T], F32, name=f"first{cb}") for cb in range(2)]
-        for cb in range(2):
-            nc.vector.tensor_copy(firsts[cb][:], dx[cb][:].indirect(pos1_sb[:]))
-        for cb, lo, hi in ((0, 0, T), (1, 0, 768), (1, 768, T)):
-            both = keep.tile([P, hi - lo], F32, name=f"both{cb}_{lo}")
-            nc.vector.tensor_tensor(both[:], dx[cb][:].indirect(pos2_sb[:, lo // LIST:hi // LIST]),
-                                    firsts[cb][:, lo:hi], ADD)
-            nc.sync.dma_start(out[cb * P:(cb + 1) * P, lo:hi], both[:])
+            first = keep.tile([P, T], F32, name=f"first{cb}")
+            pieces = ((0, 768), (768, T))
+            for lo, hi in pieces:
+                nc.vector.tensor_copy(first[:, lo:hi], dx[cb][:].indirect(pos1_sb[:, lo // LIST:hi // LIST]))
+            for lo, hi in pieces:
+                both = keep.tile([P, hi - lo], F32, name=f"both{cb}_{lo}")
+                nc.vector.tensor_tensor(both[:], dx[cb][:].indirect(pos2_sb[:, lo // LIST:hi // LIST]),
+                                        first[:, lo:hi], ADD)
+                nc.sync.dma_start(out[cb * P:(cb + 1) * P, lo:hi], both[:])

@@ -79,8 +79,8 @@ def tile_moe_qkb_kernel(
         def load_wk(e):
             nc.sync.dma_start(wk_raw[e][:], wk[e].rearrange("(p j) c -> p j c", j=4))
 
-        nc.sync.dma_start(offs_sb[:], offs)
         load_words(0, dq_words)
+        nc.sync.dma_start(offs_sb[:], offs)
         load_words(1, dk_words)
         load_words(2, dv_words)
         load_scales(0, dq_scales)
@@ -221,10 +221,9 @@ def tile_moe_qkb_kernel(
 
         for cb in range(2):
             first = keep.tile([P, T], F32, name=f"first{cb}")
-            pieces = ((0, 768), (768, T))
-            for lo, hi in pieces:
+            for lo, hi in ((0, 768), (768, T)):
                 nc.vector.tensor_copy(first[:, lo:hi], dx[cb][:].indirect(pos1_sb[:, lo // LIST:hi // LIST]))
-            for lo, hi in pieces:
+            for lo, hi in (((0, 768), (768, T)), ((0, 512), (512, 768), (768, T)))[cb]:
                 both = keep.tile([P, hi - lo], F32, name=f"both{cb}_{lo}")
                 nc.vector.tensor_tensor(both[:], dx[cb][:].indirect(pos2_sb[:, lo // LIST:hi // LIST]),
                                         first[:, lo:hi], ADD)

@@ -45,7 +45,9 @@ def tile_moe_qkb_kernel(
         w_scales = {n: keep.tile([P, E, K], U8, name=f"w{n}_scales_sb", align_bytes=64) for n in ("q", "v")}
         w_words = {(n, h): keep.tile([P, E // 2, K], I32, name=f"w{n}_words_sb{h}", align_bytes=64)
                    for n in ("q", "v") for h in range(2)}
-        wk_raw = [keep.tile([P, 4, K], F32, name=f"wk_raw{e}", tag=f"raw{e}") for e in range(E)]
+        raw_at = {4: 0, 5: 4096, 7: 12288}
+        wk_raw = [share.tile([P, 4, K], F32, name=f"wk_raw{e}", offset=raw_at[e]) if e in raw_at
+                  else keep.tile([P, 4, K], F32, name=f"wk_raw{e}") for e in range(E)]
         gate_rows = keep.tile([P, P], F32, name="gate_rows")
         gate_cols = keep.tile([P, S // P], F32, name="gate_cols")
         gate_last = keep.tile([P, S - TURNED * C], F32, name="gate_last")
@@ -105,7 +107,6 @@ def tile_moe_qkb_kernel(
         nc.tensor.transpose(gate_bank[:], gate_rows[:], identity[:])
         nc.scalar.copy(gate_cols[:], gate_bank[:, 0:S // P])
 
-        REGION = 8192
         CHUNKS = ((0, 4), (4, 6), (6, 8))
         g_words, g_scales = {}, {}
 
@@ -116,10 +117,10 @@ def tile_moe_qkb_kernel(
                     g_words[ch, i] = keep.tile([P, width], U32, name=f"g{n}w{ch}", align_bytes=64)
                     g_scales[ch, i] = keep.tile([P, width], U8, name=f"g{n}s{ch}", align_bytes=64)
                 else:
-                    base = (ch - 1) * REGION + i * 5 * width
-                    g_words[ch, i] = share.tile([P, width], U32, name=f"g{n}w{ch}", align_bytes=64, offset=base)
-                    g_scales[ch, i] = share.tile([P, width], U8, name=f"g{n}s{ch}", align_bytes=64,
-                                                 offset=base + 4 * width)
+                    words_at = (2560 * i, 10240 + (64, 3648, 5696)[i])[ch - 1]
+                    scales_at = (2560 * i + 2048, 10240 + 2112 + 512 * i)[ch - 1]
+                    g_words[ch, i] = share.tile([P, width], U32, name=f"g{n}w{ch}", align_bytes=64, offset=words_at)
+                    g_scales[ch, i] = share.tile([P, width], U8, name=f"g{n}s{ch}", align_bytes=64, offset=scales_at)
 
         def entries(ch, lo, hi):
             first = CHUNKS[ch][0] * C
@@ -138,7 +139,7 @@ def tile_moe_qkb_kernel(
         wk_codes, wk_scales, casts = {}, {}, {}
 
         def cast_half(h):
-            cast = share.tile([P, 4, K, 4], BF16, name=f"cast{h}", align_bytes=64, offset=h * REGION)
+            cast = keep.tile([P, 4, K, 4], BF16, name=f"cast{h}", align_bytes=64)
             for j in range(4):
                 nc.scalar.copy(cast[:, j], wk_raw[4 * h + j][:].rearrange("p t c -> p c t"))
             casts[h] = cast
@@ -172,7 +173,10 @@ def tile_moe_qkb_kernel(
                     ww, ws = weights(e, i, cols)
                     nc.tensor.matmul_mx(out=sums[:, blk, :], lhsT=gw, lhsT_scale=gs, rhs=ww, rhs_scale=ws,
                                         start=(i == 0), stop=(i == 2))
-            gated = keep.tile([P, 2, width], F32, name=f"gated{e}", tag=f"raw{E - 1 - e % 3}")
+            if e < 2:
+                gated = share.tile([P, 2, width], F32, name=f"gated{e}", offset=12288 + 2048 * e)
+            else:
+                gated = keep.tile([P, 2, width], F32, name=f"gated{e}")
             for blk in range(2):
                 b = 2 * e + blk
                 nc.scalar.activation(gated[:, blk, :], sums[:, blk, :], COPY, scale=gate_cols[:, b:b + 1])

@@ -20,10 +20,11 @@ ADD = mybir.AluOpType.add
 P = 128
 S = E * C
 PAIR = 2 * C
-PAIRS = E // 2
 TURNED = E - 2
 LIST = 16
+HALF = S // 2
 WIDE = 1376
+WIDEST = 4096
 
 
 def tile_moe_qkb_kernel(
@@ -39,35 +40,33 @@ def tile_moe_qkb_kernel(
         offs_sb = keep.tile([P, S // LIST], U16, name="offs_sb")
         pos1_sb = keep.tile([P, T // LIST], U16, name="pos1_sb")
         pos2_sb = keep.tile([P, T // LIST], U16, name="pos2_sb")
-        names = ("q", "k", "v")
-        d_words = [keep.tile([P, WIDE], I32, name=f"d{n}_words_sb", align_bytes=64) for n in names]
-        d_scales = [keep.tile([P, WIDE], U8, name=f"d{n}_scales_sb", align_bytes=64) for n in names]
-        w_scales = {n: keep.tile([P, E, K], U8, name=f"w{n}_scales_sb", align_bytes=64) for n in ("q", "v")}
+        d_words = {n: keep.tile([P, WIDE], I32, name=f"d{n}_words_sb", align_bytes=64) for n in "qkv"}
+        d_scales = {n: keep.tile([P, WIDEST if n == "q" else WIDE], U8, name=f"d{n}_scales_sb", align_bytes=64) for n in "qkv"}
+        w_scales = {n: keep.tile([P, E, K], U8, name=f"w{n}_scales_sb", align_bytes=64) for n in "qv"}
         w_words = {(n, h): keep.tile([P, E // 2, K], I32, name=f"w{n}_words_sb{h}", align_bytes=64)
-                   for n in ("q", "v") for h in range(2)}
-        raw_at = {4: 0, 5: 4096, 7: 12288}
-        wk_raw = [share.tile([P, 4, K], F32, name=f"wk_raw{e}", offset=raw_at[e]) if e in raw_at
-                  else keep.tile([P, 4, K], F32, name=f"wk_raw{e}") for e in range(E)]
+                   for n in "qv" for h in range(2)}
+        wv_last = [share.tile([P, P], I32, name=f"wv_last{u}", align_bytes=64, offset=18432 + 1024 * u) for u in range(2)]
+        wk_raw = [share.tile([P, 4, K], F32, name=f"wk_raw{e}", offset=14336) if e == 3
+                  else keep.tile([P, 4, K], F32, name=f"wk_raw{e}") for e in range(TURNED)]
+        wk_last = share.tile([P, 2, 4, K], F32, name="wk_last", offset=4032)
         gate_rows = keep.tile([P, P], F32, name="gate_rows")
         gate_cols = keep.tile([P, S // P], F32, name="gate_cols")
-        gate_last = keep.tile([P, S - TURNED * C], F32, name="gate_last")
+        gate_last = keep.tile([P, PAIR], F32, name="gate_last")
         identity = keep.tile([P, P], F32, name="identity")
         dx = [keep.tile([P, S], F32, name=f"dx{cb}") for cb in range(2)]
 
-        nc.vector.memset(d_words[0][:, T:], 0)
-        for plane in d_scales:
-            nc.vector.memset(plane[:].bitcast(I32), 0)
-        for table in d_words[1:]:
-            nc.vector.memset(table[:, T:], 0)
+        nc.gpsimd.memset(d_scales["q"][:, :T].bitcast(I32), 0)
+        for n in "kv":
+            nc.vector.memset(d_scales[n][:, :T].bitcast(I32), 0)
         nc.gpsimd.memset(gate_rows[:], 0.0)
         make_identity(nc, identity[:])
 
-        def load_words(i, src):
-            nc.sync.dma_start(d_words[i][:, :T], src[0].rearrange("p t d -> p (t d)").bitcast(I32))
+        def load_words(n, src):
+            nc.sync.dma_start(d_words[n][:, :T], src[0].rearrange("p t d -> p (t d)").bitcast(I32))
 
-        def load_scales(i, src):
+        def load_scales(n, src):
             for r in range(4):
-                nc.sync.dma_start(d_scales[i][r:P:32, :T].bitcast(I32), src[0].bitcast(I32)[r:16:4, :])
+                nc.sync.dma_start(d_scales[n][r:P:32, :T].bitcast(I32), src[0].bitcast(I32)[r:16:4, :])
 
         def load_w_scales(n, src):
             rows = src.rearrange("e s b c -> (s b) e c").bitcast(I32)
@@ -78,157 +77,168 @@ def tile_moe_qkb_kernel(
             half = src[4 * h: 4 * h + 4].rearrange("e s p c d -> p (e s) (c d)").bitcast(I32)
             nc.sync.dma_start(w_words[n, h][:], half)
 
-        def load_wk(e):
-            nc.sync.dma_start(wk_raw[e][:], wk[e].rearrange("(p j) c -> p j c", j=4))
-
-        load_words(0, dq_words)
         nc.sync.dma_start(offs_sb[:], offs)
-        load_words(1, dk_words)
-        load_words(2, dv_words)
-        load_scales(0, dq_scales)
-        load_wk(0)
-        load_scales(1, dk_scales)
-        load_wk(1)
-        load_scales(2, dv_scales)
-        for e in range(2, E):
-            load_wk(e)
+        nc.sync.dma_start(pos1_sb[:], pos1)
+        nc.sync.dma_start(pos2_sb[:], pos2)
+        load_scales("q", dq_scales)
+        load_words("q", dq_words)
+        for e in range(TURNED):
+            nc.sync.dma_start(wk_raw[e][:], wk[e].rearrange("(p j) c -> p j c", j=4))
+            if e == 0:
+                load_scales("k", dk_scales)
+            if e == 1:
+                load_words("k", dk_words)
+                load_scales("v", dv_scales)
+            if e == 3:
+                load_words("v", dv_words)
+        nc.sync.dma_start(wk_last[:].rearrange("p e j c -> p e (j c)"),
+                          wk[TURNED:].rearrange("e (p j) c -> p e (j c)", j=4))
         nc.sync.dma_start(gate_rows[0:S // P, :], gate[0].rearrange("(b p) -> b p", p=P))
         load_w_words("q", 0, wq_words)
         load_w_scales("q", wq_scales)
         load_w_words("v", 0, wv_words)
         load_w_scales("v", wv_scales)
         load_w_words("q", 1, wq_words)
-        load_w_words("v", 1, wv_words)
+        rows = wv_words.rearrange("e s p c d -> p (e s) (c d)").bitcast(I32)
+        nc.sync.dma_start(w_words["v", 1][:, 0:2, :], rows[:, 4:6, :])
+        for u in range(2):
+            nc.sync.dma_start(wv_last[u][:], rows[:, TURNED + u, 0:P])
+        nc.sync.dma_start(w_words["v", 1][:, 2:4, P:], rows[:, 6:8, P:])
         nc.sync.dma_start(gate_last[:], gate[:, TURNED * C:])
-        nc.sync.dma_start(pos1_sb[:], pos1)
-        nc.sync.dma_start(pos2_sb[:], pos2)
 
-        gate_bank = psum.tile([P, P], F32, name="gate_bank", tag="turn00")
+        gate_bank = psum.tile([P, P], F32, name="gate_bank", tag="b2")
         nc.tensor.transpose(gate_bank[:], gate_rows[:], identity[:])
         nc.scalar.copy(gate_cols[:], gate_bank[:, 0:S // P])
 
-        CHUNKS = ((0, 4), (4, 6), (6, 8))
-        g_words, g_scales = {}, {}
+        casts = [keep.tile([P, 4, K, 4], BF16, name="cast0", align_bytes=64),
+                 keep.tile([P, 3, K, 4], BF16, name="cast1", align_bytes=64),
+                 keep.tile([P, 1, P, 4], BF16, name="cast2", align_bytes=64),
+                 keep.tile([P, 1, P, 4], BF16, name="cast3", align_bytes=64)]
+        for e in range(TURNED):
+            nc.scalar.copy(casts[e // 4][:, e % 4], wk_raw[e][:].rearrange("p t c -> p c t"))
+        nc.scalar.copy(casts[1][:, 2].rearrange("p (e c) t -> p e c t", e=2),
+                       wk_last[:, :, :, 0:P].rearrange("p e t c -> p e c t"))
+        for u in range(2):
+            nc.scalar.copy(casts[2 + u][:, 0], wk_last[:, u, :, P:].rearrange("p t c -> p c t"))
 
-        def gathered_tiles(ch):
-            width = (CHUNKS[ch][1] - CHUNKS[ch][0]) * C
-            for i, n in enumerate(names):
-                if ch == 0:
-                    g_words[ch, i] = keep.tile([P, width], U32, name=f"g{n}w{ch}", align_bytes=64)
-                    g_scales[ch, i] = keep.tile([P, width], U8, name=f"g{n}s{ch}", align_bytes=64)
-                else:
-                    words_at = (2560 * i, 10240 + (64, 3648, 5696)[i])[ch - 1]
-                    scales_at = (2560 * i + 2048, 10240 + 2112 + 512 * i)[ch - 1]
-                    g_words[ch, i] = share.tile([P, width], U32, name=f"g{n}w{ch}", align_bytes=64, offset=words_at)
-                    g_scales[ch, i] = share.tile([P, width], U8, name=f"g{n}s{ch}", align_bytes=64, offset=scales_at)
+        pieces = {}
 
-        def entries(ch, lo, hi):
-            first = CHUNKS[ch][0] * C
-            return offs_sb[:, (first + lo) // LIST:(first + hi) // LIST]
+        def gathered(kind, n, lo, hi, offset=None):
+            dtype = U32 if kind == "w" else U8
+            if offset is None:
+                piece = keep.tile([P, hi - lo], dtype, name=f"g{n}{kind}{lo}", align_bytes=64)
+            else:
+                piece = share.tile([P, hi - lo], dtype, name=f"g{n}{kind}{lo}", align_bytes=64, offset=offset)
+            pieces.setdefault((kind, n), []).append((lo, hi, piece))
+            window = d_words[n][:].bitcast(U32) if kind == "w" else d_scales[n][:]
+            nc.vector.tensor_copy(piece[:], window.indirect(offs_sb[:, lo // LIST:hi // LIST]))
 
-        def gather_words(ch, i, lo, hi):
-            nc.vector.tensor_copy(g_words[ch, i][:, lo:hi], d_words[i][:].bitcast(U32).indirect(entries(ch, lo, hi)))
+        def slots(kind, n, lo, hi):
+            return [piece[:, lo - a:hi - a] for a, b, piece in pieces[kind, n] if a <= lo and hi <= b][0]
 
-        def gather_scales(ch, i, lo, hi):
-            nc.vector.tensor_copy(g_scales[ch, i][:, lo:hi], d_scales[i][:].indirect(entries(ch, lo, hi)))
+        wk_codes = [keep.tile([P, 4, K], U32, name="wk_codes0", align_bytes=64),
+                    keep.tile([P, 3, K], U32, name="wk_codes1", align_bytes=64),
+                    share.tile([P, 1, P], U32, name="wk_codes2", align_bytes=64, offset=18432),
+                    share.tile([P, 1, P], U32, name="wk_codes3", align_bytes=64, offset=19456)]
+        wk_scales = [keep.tile([P, 4, K], U8, name="wk_scales0", align_bytes=64),
+                     keep.tile([P, 3, K], U8, name="wk_scales1", align_bytes=64),
+                     keep.tile([P, 1, P], U8, name="wk_scales2", align_bytes=64),
+                     keep.tile([P, 1, P], U8, name="wk_scales3", align_bytes=64)]
 
-        def gather(ch, i, lo, hi):
-            gather_words(ch, i, lo, hi)
-            gather_scales(ch, i, lo, hi)
+        def quantise(h, lo, hi):
+            nc.vector.quantize_mx(out=wk_codes[h][:, lo:hi].rearrange("p j c -> p (j c)").bitcast(FP8X4),
+                                  scales=wk_scales[h][:, lo:hi].rearrange("p j c -> p (j c)"),
+                                  in_=casts[h][:, lo:hi].rearrange("p j c t -> p (j c t)"))
 
-        wk_codes, wk_scales, casts = {}, {}, {}
-
-        def cast_half(h):
-            cast = keep.tile([P, 4, K, 4], BF16, name=f"cast{h}", align_bytes=64)
-            for j in range(4):
-                nc.scalar.copy(cast[:, j], wk_raw[4 * h + j][:].rearrange("p t c -> p c t"))
-            casts[h] = cast
-
-        def quantise_half(h):
-            wk_codes[h] = keep.tile([P, 4, K], U32, name=f"wk_codes{h}", align_bytes=64)
-            wk_scales[h] = keep.tile([P, 4, K], U8, name=f"wk_scales{h}", align_bytes=64)
-            nc.vector.quantize_mx(out=wk_codes[h][:].rearrange("p j c -> p (j c)").bitcast(FP8X4),
-                                  scales=wk_scales[h][:].rearrange("p j c -> p (j c)"),
-                                  in_=casts[h][:].rearrange("p j c t -> p (j c t)"))
-
-        def weights(e, i, cols):
-            if i == 1:
+        def weights(e, n, cols):
+            if n == "k" and e < TURNED:
                 return wk_codes[e // 4][:, e % 4, cols].bitcast(FP8X4), wk_scales[e // 4][:, e % 4, cols]
-            n = names[i]
+            if n == "k" and cols.start == 0:
+                mine = slice((e - TURNED) * P, (e - TURNED + 1) * P)
+                return wk_codes[1][:, 2, mine].bitcast(FP8X4), wk_scales[1][:, 2, mine]
+            if n == "k":
+                return wk_codes[e - 4][:, 0, :].bitcast(FP8X4), wk_scales[e - 4][:, 0, :]
+            if n == "v" and e >= TURNED and cols.start == 0:
+                return wv_last[e - TURNED][:].bitcast(FP8X4), w_scales[n][:, e, cols]
             return w_words[n, e // 4][:, e % 4, cols].bitcast(FP8X4), w_scales[n][:, e, cols]
 
-        def grads(e, i, lo, hi):
-            ch = max(0, e // 2 - 1)
-            first = (e - CHUNKS[ch][0]) * C
-            cols = slice(first + lo, first + hi)
-            return g_words[ch, i][:, cols].bitcast(FP8X4), g_scales[ch, i][:, cols]
+        def grads(n, lo, hi):
+            return slots("w", n, lo, hi).bitcast(FP8X4), slots("s", n, lo, hi)
 
-        def turned(e, cbs, sums_tag, turn_tags):
+        def turned(pair, cbs, sums_tags, turn_tags, order="qkv"):
             cols = slice(cbs[0] * P, (cbs[-1] + 1) * P)
             width = len(cbs) * P
-            sums = psum.tile([P, 2, width], F32, name=f"sums{e}", tag=sums_tag)
-            for blk in range(2):
-                for i in range(3):
-                    gw, gs = grads(e, i, blk * P, (blk + 1) * P)
-                    ww, ws = weights(e, i, cols)
-                    nc.tensor.matmul_mx(out=sums[:, blk, :], lhsT=gw, lhsT_scale=gs, rhs=ww, rhs_scale=ws,
-                                        start=(i == 0), stop=(i == 2))
-            if e < 2:
-                gated = share.tile([P, 2, width], F32, name=f"gated{e}", offset=12288 + 2048 * e)
+            gated = keep.tile([P, 4, width], F32, name=f"gated{pair}_{cbs[0]}")
+            if len(sums_tags) == 4:
+                sums = [psum.tile([P, width], F32, name=f"sums{pair}_{cbs[0]}_{b}", tag=tag)[:] for b, tag in enumerate(sums_tags)]
+                passes = [(b, n) for n in order for b in range(4)]
             else:
-                gated = keep.tile([P, 2, width], F32, name=f"gated{e}")
-            for blk in range(2):
-                b = 2 * e + blk
-                nc.scalar.activation(gated[:, blk, :], sums[:, blk, :], COPY, scale=gate_cols[:, b:b + 1])
-            turns = [psum.tile([P, C], F32, name=f"turn{e}_{cb}", tag=tag) for cb, tag in zip(cbs, turn_tags)]
-            for blk in range(2):
-                for j in range(len(cbs)):
-                    nc.tensor.transpose(turns[j][:, blk * P:(blk + 1) * P], gated[:, blk, j * P:(j + 1) * P], identity[:])
+                banks = [psum.tile([P, 2, width], F32, name=f"sums{pair}_{cbs[0]}_{u}", tag=tag) for u, tag in enumerate(sums_tags)]
+                sums = [banks[b // 2][:, b % 2, :] for b in range(4)]
+                passes = [(b, n) for b in range(4) for n in order]
+            for b, n in passes:
+                lo = pair * PAIR + b * P
+                gw, gs = grads(n, lo, lo + P)
+                ww, ws = weights(2 * pair + b // 2, n, cols)
+                nc.tensor.matmul_mx(out=sums[b], lhsT=gw, lhsT_scale=gs, rhs=ww, rhs_scale=ws,
+                                    start=(n == order[0]), stop=(n == order[-1]))
+            for b in range(4):
+                nc.scalar.activation(gated[:, b, :], sums[b], COPY, scale=gate_cols[:, 4 * pair + b:4 * pair + b + 1])
+            parts = len(turn_tags) // len(cbs)
+            blocks = 4 // parts
             for j, cb in enumerate(cbs):
-                nc.scalar.copy(dx[cb][:, e * C:(e + 1) * C], turns[j][:])
+                for part in range(parts):
+                    turn = psum.tile([P, blocks * P], F32, name=f"turn{pair}_{cb}_{part}", tag=turn_tags[j * parts + part])
+                    for b in range(blocks):
+                        nc.tensor.transpose(turn[:, b * P:(b + 1) * P],
+                                            gated[:, part * blocks + b, j * P:(j + 1) * P], identity[:])
+                    lo = pair * PAIR + part * blocks * P
+                    nc.scalar.copy(dx[cb][:, lo:lo + blocks * P], turn[:])
 
-        def direct_sums(e, tag):
-            sums = psum.tile([P, C], F32, name=f"direct{e}", tag=tag)
-            for i in range(3):
-                gw, gs = grads(e, i, 0, C)
-                ww, ws = weights(e, i, slice(0, P))
-                nc.tensor.matmul_mx(out=sums[:], lhsT=ww, lhsT_scale=ws, rhs=gw, rhs_scale=gs,
-                                    start=(i == 0), stop=(i == 2))
-            nc.vector.tensor_tensor(dx[0][:, e * C:(e + 1) * C], sums[:],
-                                    gate_last[:, (e - TURNED) * C:(e - TURNED + 1) * C], MULT)
+        def direct(tags):
+            sums = [psum.tile([P, C], F32, name=f"direct{u}", tag=tag) for u, tag in enumerate(tags)]
+            for u, n in ((0, "q"), (0, "k"), (1, "q"), (1, "k"), (0, "v"), (1, "v")):
+                e = TURNED + u
+                gw, gs = grads(n, e * C, (e + 1) * C)
+                ww, ws = weights(e, n, slice(0, P))
+                nc.tensor.matmul_mx(out=sums[u][:], lhsT=ww, lhsT_scale=ws, rhs=gw, rhs_scale=gs,
+                                    start=(n == "q"), stop=(n == "v"))
+            for u in range(2):
+                e = TURNED + u
+                nc.vector.tensor_tensor(dx[0][:, e * C:(e + 1) * C], sums[u][:], gate_last[:, u * C:(u + 1) * C], MULT)
+                quantise(2 + u, 0, 1)
 
-        cast_half(0)
-        cast_half(1)
-        gathered_tiles(0)
-        for i in range(3):
-            gather_words(0, i, 0, 4 * C)
-        for i in range(3):
-            gather_scales(0, i, 0, 4 * C)
-        quantise_half(0)
-        gathered_tiles(1)
-        for i in range(3):
-            gather(1, i, 0, PAIR)
-        for e in range(4):
-            turned(e, (0, 1), f"sums{e % 2}", (f"turn{e % 2}0", f"turn{e % 2}1"))
-        quantise_half(1)
-        gathered_tiles(2)
-        for i in range(2):
-            gather(2, i, 0, PAIR)
-        for j in range(2):
-            gather(2, 2, j * C, (j + 1) * C)
-        for e in (4, 5):
-            turned(e, (0, 1), f"sums{e % 2}", (f"turn{e % 2}0", f"turn{e % 2}1"))
-        direct_sums(6, "sums1")
-        direct_sums(7, "turn11")
-        turned(6, (1,), "turn10", ("turn00",))
-        turned(7, (1,), "turn10", ("turn01",))
+        gathered("s", "q", 0, S)
+        gathered("w", "q", 0, HALF)
+        gathered("w", "k", 0, HALF)
+        gathered("s", "k", 0, HALF)
+        gathered("w", "v", 0, HALF)
+        quantise(0, 0, 4)
+        gathered("s", "v", 0, HALF, 14336)
+        gathered("w", "q", HALF, S, 0)
+        quantise(1, 0, 2)
+        quantise(1, 2, 3)
+        gathered("s", "k", HALF, HALF + PAIR, 15360)
+        gathered("w", "k", HALF, HALF + PAIR, 5120)
+        gathered("w", "v", HALF, HALF + PAIR, 7168)
+        gathered("s", "v", HALF, HALF + PAIR, 9216)
+        gathered("s", "k", HALF + PAIR, S, 4352)
+        gathered("w", "k", HALF + PAIR, S, 9728)
+        gathered("w", "v", HALF + PAIR, S, 12160)
+        gathered("s", "v", 6 * C, 7 * C, 11776)
+        gathered("s", "v", 7 * C, 8 * C, 4096)
+        turned(0, (0, 1), ("b0", "b1"), ("b2", "b3"))
+        turned(1, (0, 1), ("b4", "b5"), ("b2", "b3", "b6", "b7"))
+        turned(2, (0, 1), ("b2", "b3", "b6", "b7"), ("b0", "b1", "b4", "b5"))
+        direct(("b6", "b7"))
+        turned(3, (1,), ("b0", "b1", "b4", "b5"), ("b2", "b3"), "qvk")
 
+        first = [keep.tile([P, T], F32, name=f"first{cb}") for cb in range(2)]
         for cb in range(2):
-            first = keep.tile([P, T], F32, name=f"first{cb}")
-            for lo, hi in ((0, 768), (768, T)):
-                nc.vector.tensor_copy(first[:, lo:hi], dx[cb][:].indirect(pos1_sb[:, lo // LIST:hi // LIST]))
-            for lo, hi in (((0, 768), (768, T)), ((0, 512), (512, 768), (768, T)))[cb]:
+            for lo, hi in ((0, 512), (512, T)):
+                nc.vector.tensor_copy(first[cb][:, lo:hi], dx[cb][:].indirect(pos1_sb[:, lo // LIST:hi // LIST]))
+            for lo, hi in (((0, 512), (512, T)), ((0, 512), (512, 896), (896, T)))[cb]:
                 both = keep.tile([P, hi - lo], F32, name=f"both{cb}_{lo}")
                 nc.vector.tensor_tensor(both[:], dx[cb][:].indirect(pos2_sb[:, lo // LIST:hi // LIST]),
-                                        first[:, lo:hi], ADD)
+                                        first[cb][:, lo:hi], ADD)
                 nc.sync.dma_start(out[cb * P:(cb + 1) * P, lo:hi], both[:])

@@ -45,7 +45,6 @@ def tile_moe_qkb_kernel(
         w_scales = {n: keep.tile([P, E, K], U8, name=f"w{n}_scales_sb", align_bytes=64) for n in "qv"}
         w_words = {(n, h): keep.tile([P, E // 2, K], I32, name=f"w{n}_words_sb{h}", align_bytes=64)
                    for n in "qv" for h in range(2)}
-        wv_last = [share.tile([P, P], I32, name=f"wv_last{u}", align_bytes=64, offset=18432 + 1024 * u) for u in range(2)]
         wk_raw = [share.tile([P, 4, K], F32, name=f"wk_raw{e}", offset=14336) if e == 3
                   else keep.tile([P, 4, K], F32, name=f"wk_raw{e}") for e in range(TURNED)]
         wk_last = share.tile([P, 2, 4, K], F32, name="wk_last", offset=4032)
@@ -99,11 +98,7 @@ def tile_moe_qkb_kernel(
         load_w_words("v", 0, wv_words)
         load_w_scales("v", wv_scales)
         load_w_words("q", 1, wq_words)
-        rows = wv_words.rearrange("e s p c d -> p (e s) (c d)").bitcast(I32)
-        nc.sync.dma_start(w_words["v", 1][:, 0:2, :], rows[:, 4:6, :])
-        for u in range(2):
-            nc.sync.dma_start(wv_last[u][:], rows[:, TURNED + u, 0:P])
-        nc.sync.dma_start(w_words["v", 1][:, 2:4, P:], rows[:, 6:8, P:])
+        load_w_words("v", 1, wv_words)
         nc.sync.dma_start(gate_last[:], gate[:, TURNED * C:])
 
         gate_bank = psum.tile([P, P], F32, name="gate_bank", tag="b2")
@@ -112,14 +107,13 @@ def tile_moe_qkb_kernel(
 
         casts = [keep.tile([P, 4, K, 4], BF16, name="cast0", align_bytes=64),
                  keep.tile([P, 3, K, 4], BF16, name="cast1", align_bytes=64),
-                 keep.tile([P, 1, P, 4], BF16, name="cast2", align_bytes=64),
-                 keep.tile([P, 1, P, 4], BF16, name="cast3", align_bytes=64)]
+                 keep.tile([P, 1, K, 4], BF16, name="cast2", align_bytes=64)]
         for e in range(TURNED):
             nc.scalar.copy(casts[e // 4][:, e % 4], wk_raw[e][:].rearrange("p t c -> p c t"))
         nc.scalar.copy(casts[1][:, 2].rearrange("p (e c) t -> p e c t", e=2),
                        wk_last[:, :, :, 0:P].rearrange("p e t c -> p e c t"))
-        for u in range(2):
-            nc.scalar.copy(casts[2 + u][:, 0], wk_last[:, u, :, P:].rearrange("p t c -> p c t"))
+        nc.scalar.copy(casts[2][:, 0].rearrange("p (e c) t -> p e c t", e=2),
+                       wk_last[:, :, :, P:].rearrange("p e t c -> p e c t"))
 
         pieces = {}
 
@@ -138,12 +132,10 @@ def tile_moe_qkb_kernel(
 
         wk_codes = [keep.tile([P, 4, K], U32, name="wk_codes0", align_bytes=64),
                     keep.tile([P, 3, K], U32, name="wk_codes1", align_bytes=64),
-                    share.tile([P, 1, P], U32, name="wk_codes2", align_bytes=64, offset=18432),
-                    share.tile([P, 1, P], U32, name="wk_codes3", align_bytes=64, offset=19456)]
+                    keep.tile([P, 1, K], U32, name="wk_codes2", align_bytes=64)]
         wk_scales = [keep.tile([P, 4, K], U8, name="wk_scales0", align_bytes=64),
                      keep.tile([P, 3, K], U8, name="wk_scales1", align_bytes=64),
-                     keep.tile([P, 1, P], U8, name="wk_scales2", align_bytes=64),
-                     keep.tile([P, 1, P], U8, name="wk_scales3", align_bytes=64)]
+                     keep.tile([P, 1, K], U8, name="wk_scales2", align_bytes=64)]
 
         def quantise(h, lo, hi):
             nc.vector.quantize_mx(out=wk_codes[h][:, lo:hi].rearrange("p j c -> p (j c)").bitcast(FP8X4),
@@ -153,13 +145,10 @@ def tile_moe_qkb_kernel(
         def weights(e, n, cols):
             if n == "k" and e < TURNED:
                 return wk_codes[e // 4][:, e % 4, cols].bitcast(FP8X4), wk_scales[e // 4][:, e % 4, cols]
-            if n == "k" and cols.start == 0:
-                mine = slice((e - TURNED) * P, (e - TURNED + 1) * P)
-                return wk_codes[1][:, 2, mine].bitcast(FP8X4), wk_scales[1][:, 2, mine]
             if n == "k":
-                return wk_codes[e - 4][:, 0, :].bitcast(FP8X4), wk_scales[e - 4][:, 0, :]
-            if n == "v" and e >= TURNED and cols.start == 0:
-                return wv_last[e - TURNED][:].bitcast(FP8X4), w_scales[n][:, e, cols]
+                mine = slice((e - TURNED) * P, (e - TURNED + 1) * P)
+                h, j = (1, 2) if cols.start == 0 else (2, 0)
+                return wk_codes[h][:, j, mine].bitcast(FP8X4), wk_scales[h][:, j, mine]
             return w_words[n, e // 4][:, e % 4, cols].bitcast(FP8X4), w_scales[n][:, e, cols]
 
         def grads(n, lo, hi):
@@ -196,17 +185,19 @@ def tile_moe_qkb_kernel(
                     nc.scalar.copy(dx[cb][:, lo:lo + blocks * P], turn[:])
 
         def direct(tags):
-            sums = [psum.tile([P, C], F32, name=f"direct{u}", tag=tag) for u, tag in enumerate(tags)]
-            for u, n in ((0, "q"), (0, "k"), (1, "q"), (1, "k"), (0, "v"), (1, "v")):
+            sums = {(u, cb): psum.tile([P, C], F32, name=f"direct{u}_{cb}", tag=tags[2 * cb + u])
+                    for cb in range(2) for u in range(2)}
+            early = [(u, cb, n) for cb in range(2) for u in range(2) for n in "qv"]
+            late = [(u, cb, "k") for cb in range(2) for u in range(2)]
+            for u, cb, n in early + late:
                 e = TURNED + u
                 gw, gs = grads(n, e * C, (e + 1) * C)
-                ww, ws = weights(e, n, slice(0, P))
-                nc.tensor.matmul_mx(out=sums[u][:], lhsT=ww, lhsT_scale=ws, rhs=gw, rhs_scale=gs,
-                                    start=(n == "q"), stop=(n == "v"))
-            for u in range(2):
+                ww, ws = weights(e, n, slice(cb * P, (cb + 1) * P))
+                nc.tensor.matmul_mx(out=sums[u, cb][:], lhsT=ww, lhsT_scale=ws, rhs=gw, rhs_scale=gs,
+                                    start=(n == "q"), stop=(n == "k"))
+            for u, cb, n in late:
                 e = TURNED + u
-                nc.vector.tensor_tensor(dx[0][:, e * C:(e + 1) * C], sums[u][:], gate_last[:, u * C:(u + 1) * C], MULT)
-                quantise(2 + u, 0, 1)
+                nc.vector.tensor_tensor(dx[cb][:, e * C:(e + 1) * C], sums[u, cb][:], gate_last[:, u * C:(u + 1) * C], MULT)
 
         gathered("s", "q", 0, S)
         gathered("w", "q", 0, HALF)
@@ -222,23 +213,31 @@ def tile_moe_qkb_kernel(
         gathered("w", "k", HALF, HALF + PAIR, 5120)
         gathered("w", "v", HALF, HALF + PAIR, 7168)
         gathered("s", "v", HALF, HALF + PAIR, 9216)
-        gathered("s", "k", HALF + PAIR, S, 4352)
-        gathered("w", "k", HALF + PAIR, S, 9728)
-        gathered("w", "v", HALF + PAIR, S, 12160)
-        gathered("s", "v", 6 * C, 7 * C, 11776)
-        gathered("s", "v", 7 * C, 8 * C, 4096)
+        gathered("s", "v", HALF + PAIR, S, 4352)
+        gathered("w", "v", HALF + PAIR, S, 9728)
+        gathered("w", "k", HALF + PAIR, S, 12160)
+        gathered("s", "k", 6 * C, 7 * C, 11776)
+        gathered("s", "k", 7 * C, 8 * C, 4096)
+        quantise(2, 0, 1)
         turned(0, (0, 1), ("b0", "b1"), ("b2", "b3"))
         turned(1, (0, 1), ("b4", "b5"), ("b2", "b3", "b6", "b7"))
         turned(2, (0, 1), ("b2", "b3", "b6", "b7"), ("b0", "b1", "b4", "b5"))
-        direct(("b6", "b7"))
-        turned(3, (1,), ("b0", "b1", "b4", "b5"), ("b2", "b3"), "qvk")
+        direct(("b6", "b7", "b0", "b1"))
 
-        first = [keep.tile([P, T], F32, name=f"first{cb}") for cb in range(2)]
+        fetch = 256
+        stores = (((0, 512), (512, T)), ((0, 512), (512, 896), (896, T)))
         for cb in range(2):
-            for lo, hi in ((0, 512), (512, T)):
-                nc.vector.tensor_copy(first[cb][:, lo:hi], dx[cb][:].indirect(pos1_sb[:, lo // LIST:hi // LIST]))
-            for lo, hi in (((0, 512), (512, T)), ((0, 512), (512, 896), (896, T)))[cb]:
+            first = {}
+            for lo in range(0, T, fetch):
+                first[lo] = keep.tile([P, fetch], F32, name=f"first{cb}_{lo}")
+                nc.scalar.activation(first[lo][:], dx[cb][:].indirect(pos1_sb[:, lo // LIST:(lo + fetch) // LIST]), COPY)
+            for lo, hi in stores[cb]:
                 both = keep.tile([P, hi - lo], F32, name=f"both{cb}_{lo}")
-                nc.vector.tensor_tensor(both[:], dx[cb][:].indirect(pos2_sb[:, lo // LIST:hi // LIST]),
-                                        first[cb][:, lo:hi], ADD)
+                a = lo
+                while a < hi:
+                    base = a - a % fetch
+                    b = min(hi, base + fetch)
+                    nc.vector.tensor_tensor(both[:, a - lo:b - lo], dx[cb][:].indirect(pos2_sb[:, a // LIST:b // LIST]),
+                                            first[base][:, a - base:b - base], ADD)
+                    a = b
                 nc.sync.dma_start(out[cb * P:(cb + 1) * P, lo:hi], both[:])

@@ -23,8 +23,13 @@ PAIR = 2 * C
 TURNED = E - 2
 LIST = 16
 HALF = S // 2
+LAST = TURNED * C
 WIDE = 1376
 WIDEST = 4096
+WHOLE = E // 2
+RAW3_AT = 16384
+GATED1_AT = 20480
+GATED2_AT = 24576
 
 
 def tile_moe_qkb_kernel(
@@ -40,17 +45,19 @@ def tile_moe_qkb_kernel(
         offs_sb = keep.tile([P, S // LIST], U16, name="offs_sb")
         pos1_sb = keep.tile([P, T // LIST], U16, name="pos1_sb")
         pos2_sb = keep.tile([P, T // LIST], U16, name="pos2_sb")
-        d_words = {n: keep.tile([P, WIDE], I32, name=f"d{n}_words_sb", align_bytes=64) for n in "qkv"}
-        d_scales = {n: keep.tile([P, WIDEST if n == "q" else WIDE], U8, name=f"d{n}_scales_sb", align_bytes=64) for n in "qkv"}
+        window = {"q": WIDEST, "k": WIDE, "v": WIDE}
+        d_words = {n: keep.tile([P, window[n]], I32, name=f"d{n}_words_sb", align_bytes=64) for n in "qkv"}
+        d_scales = {n: keep.tile([P, window[n]], U8, name=f"d{n}_scales_sb", align_bytes=64) for n in "qkv"}
         w_scales = {n: keep.tile([P, E, K], U8, name=f"w{n}_scales_sb", align_bytes=64) for n in "qv"}
-        w_words = {(n, h): keep.tile([P, E // 2, K], I32, name=f"w{n}_words_sb{h}", align_bytes=64)
-                   for n in "qv" for h in range(2)}
-        wk_raw = [share.tile([P, 4, K], F32, name=f"wk_raw{e}", offset=14336) if e == 3
-                  else keep.tile([P, 4, K], F32, name=f"wk_raw{e}") for e in range(TURNED)]
-        wk_last = share.tile([P, 2, 4, K], F32, name="wk_last", offset=4032)
+        w_words = {(n, pair): keep.tile([P, 2, K], I32, name=f"w{n}_words_sb{pair}", align_bytes=64)
+                   for n in "qv" for pair in range(E // 2) if n == "q" or pair < WHOLE // 2}
+        wv_late = [keep.tile([P, E - WHOLE, P], I32, name="wv_late0", align_bytes=64)]
+        wk_raw = [share.tile([P, 4, K], F32, name=f"wk_raw{e}", offset=RAW3_AT) if e == 3
+                  else keep.tile([P, 4, K], F32, name=f"wk_raw{e}") for e in range(WHOLE)]
+        wk_late = share.tile([P, E - WHOLE, 4, K], F32, name="wk_late", offset=0)
         gate_rows = keep.tile([P, P], F32, name="gate_rows")
         gate_cols = keep.tile([P, S // P], F32, name="gate_cols")
-        gate_last = keep.tile([P, PAIR], F32, name="gate_last")
+        gate_late = keep.tile([P, HALF], F32, name="gate_late")
         identity = keep.tile([P, P], F32, name="identity")
         dx = [keep.tile([P, S], F32, name=f"dx{cb}") for cb in range(2)]
 
@@ -67,53 +74,62 @@ def tile_moe_qkb_kernel(
             for r in range(4):
                 nc.sync.dma_start(d_scales[n][r:P:32, :T].bitcast(I32), src[0].bitcast(I32)[r:16:4, :])
 
+        def load_wk(e):
+            nc.sync.dma_start(wk_raw[e][:], wk[e].rearrange("(p j) c -> p j c", j=4))
+
         def load_w_scales(n, src):
             rows = src.rearrange("e s b c -> (s b) e c").bitcast(I32)
             for r in range(4):
                 nc.sync.dma_start(w_scales[n][r:P:32, :, :].bitcast(I32), rows[r:16:4, :, :])
 
-        def load_w_words(n, h, src):
-            half = src[4 * h: 4 * h + 4].rearrange("e s p c d -> p (e s) (c d)").bitcast(I32)
-            nc.sync.dma_start(w_words[n, h][:], half)
+        def load_w_words(n, pair, src):
+            two = src[2 * pair:2 * pair + 2].rearrange("e s p c d -> p (e s) (c d)").bitcast(I32)
+            nc.sync.dma_start(w_words[n, pair][:], two)
 
         nc.sync.dma_start(offs_sb[:], offs)
         nc.sync.dma_start(pos1_sb[:], pos1)
         nc.sync.dma_start(pos2_sb[:], pos2)
         load_scales("q", dq_scales)
         load_words("q", dq_words)
-        for e in range(TURNED):
-            nc.sync.dma_start(wk_raw[e][:], wk[e].rearrange("(p j) c -> p j c", j=4))
-            if e == 0:
-                load_scales("k", dk_scales)
-            if e == 1:
-                load_words("k", dk_words)
-                load_scales("v", dv_scales)
-            if e == 3:
-                load_words("v", dv_words)
-        nc.sync.dma_start(wk_last[:].rearrange("p e j c -> p e (j c)"),
-                          wk[TURNED:].rearrange("e (p j) c -> p e (j c)", j=4))
+        load_wk(0)
+        load_scales("k", dk_scales)
+        load_wk(1)
+        load_words("k", dk_words)
+        load_scales("v", dv_scales)
+        load_wk(2)
+        load_wk(3)
+        load_words("v", dv_words)
+        for e in range(WHOLE, E, 2):
+            nc.sync.dma_start(wk_late[:, e - WHOLE:e - WHOLE + 2].rearrange("p e j c -> p e (j c)"),
+                              wk[e:e + 2].rearrange("e (p j) c -> p e (j c)", j=4))
         nc.sync.dma_start(gate_rows[0:S // P, :], gate[0].rearrange("(b p) -> b p", p=P))
-        load_w_words("q", 0, wq_words)
-        load_w_scales("q", wq_scales)
-        load_w_words("v", 0, wv_words)
-        load_w_scales("v", wv_scales)
-        load_w_words("q", 1, wq_words)
-        load_w_words("v", 1, wv_words)
-        nc.sync.dma_start(gate_last[:], gate[:, TURNED * C:])
+        for n, words, scales in (("q", wq_words, wq_scales), ("v", wv_words, wv_scales)):
+            load_w_words(n, 0, words)
+            load_w_scales(n, scales)
+            load_w_words(n, 1, words)
+        for pair in range(2, E // 2):
+            load_w_words("q", pair, wq_words)
+        wv_rows = wv_words[WHOLE:].rearrange("e s p c d -> p (e s) (c d)").bitcast(I32)
+        nc.sync.dma_start(wv_late[0][:], wv_rows[:, :, 0:P])
+        nc.sync.dma_start(gate_late[:], gate[:, HALF:])
 
         gate_bank = psum.tile([P, P], F32, name="gate_bank", tag="b2")
         nc.tensor.transpose(gate_bank[:], gate_rows[:], identity[:])
         nc.scalar.copy(gate_cols[:], gate_bank[:, 0:S // P])
 
-        casts = [keep.tile([P, 4, K, 4], BF16, name="cast0", align_bytes=64),
-                 keep.tile([P, 3, K, 4], BF16, name="cast1", align_bytes=64),
-                 keep.tile([P, 1, K, 4], BF16, name="cast2", align_bytes=64)]
-        for e in range(TURNED):
-            nc.scalar.copy(casts[e // 4][:, e % 4], wk_raw[e][:].rearrange("p t c -> p c t"))
-        nc.scalar.copy(casts[1][:, 2].rearrange("p (e c) t -> p e c t", e=2),
-                       wk_last[:, :, :, 0:P].rearrange("p e t c -> p e c t"))
-        nc.scalar.copy(casts[2][:, 0].rearrange("p (e c) t -> p e c t", e=2),
-                       wk_last[:, :, :, P:].rearrange("p e t c -> p e c t"))
+        widths = (WHOLE * K, WHOLE * P, WHOLE * P)
+        casts = [keep.tile([P, w, 4], BF16, name=f"cast{h}", align_bytes=64) for h, w in enumerate(widths)]
+        wk_codes = [keep.tile([P, w], U32, name=f"wk_codes{h}", align_bytes=64) for h, w in enumerate(widths[:2])]
+        wk_scales = [keep.tile([P, w], U8, name=f"wk_scales{h}", align_bytes=64) for h, w in enumerate(widths)]
+        for e in range(WHOLE):
+            nc.scalar.copy(casts[0][:, e * K:(e + 1) * K], wk_raw[e][:].rearrange("p t c -> p c t"))
+        for cb in range(2):
+            nc.scalar.copy(casts[1 + cb][:].rearrange("p (e c) t -> p e c t", e=E - WHOLE),
+                           wk_late[:, :, :, cb * P:(cb + 1) * P].rearrange("p e t c -> p e c t"))
+
+        def quantise(h):
+            nc.vector.quantize_mx(out=wk_codes[h][:].bitcast(FP8X4), scales=wk_scales[h][:],
+                                  in_=casts[h][:].rearrange("p c t -> p (c t)"))
 
         pieces = {}
 
@@ -124,120 +140,103 @@ def tile_moe_qkb_kernel(
             else:
                 piece = share.tile([P, hi - lo], dtype, name=f"g{n}{kind}{lo}", align_bytes=64, offset=offset)
             pieces.setdefault((kind, n), []).append((lo, hi, piece))
-            window = d_words[n][:].bitcast(U32) if kind == "w" else d_scales[n][:]
-            nc.vector.tensor_copy(piece[:], window.indirect(offs_sb[:, lo // LIST:hi // LIST]))
+            table = d_words[n][:].bitcast(U32) if kind == "w" else d_scales[n][:]
+            nc.vector.tensor_copy(piece[:], table.indirect(offs_sb[:, lo // LIST:hi // LIST]))
 
         def slots(kind, n, lo, hi):
             return [piece[:, lo - a:hi - a] for a, b, piece in pieces[kind, n] if a <= lo and hi <= b][0]
 
-        wk_codes = [keep.tile([P, 4, K], U32, name="wk_codes0", align_bytes=64),
-                    keep.tile([P, 3, K], U32, name="wk_codes1", align_bytes=64),
-                    keep.tile([P, 1, K], U32, name="wk_codes2", align_bytes=64)]
-        wk_scales = [keep.tile([P, 4, K], U8, name="wk_scales0", align_bytes=64),
-                     keep.tile([P, 3, K], U8, name="wk_scales1", align_bytes=64),
-                     keep.tile([P, 1, K], U8, name="wk_scales2", align_bytes=64)]
-
-        def quantise(h, lo, hi):
-            nc.vector.quantize_mx(out=wk_codes[h][:, lo:hi].rearrange("p j c -> p (j c)").bitcast(FP8X4),
-                                  scales=wk_scales[h][:, lo:hi].rearrange("p j c -> p (j c)"),
-                                  in_=casts[h][:, lo:hi].rearrange("p j c t -> p (j c t)"))
-
-        def weights(e, n, cols):
-            if n == "k" and e < TURNED:
-                return wk_codes[e // 4][:, e % 4, cols].bitcast(FP8X4), wk_scales[e // 4][:, e % 4, cols]
-            if n == "k":
-                mine = slice((e - TURNED) * P, (e - TURNED + 1) * P)
-                h, j = (1, 2) if cols.start == 0 else (2, 0)
-                return wk_codes[h][:, j, mine].bitcast(FP8X4), wk_scales[h][:, j, mine]
-            return w_words[n, e // 4][:, e % 4, cols].bitcast(FP8X4), w_scales[n][:, e, cols]
-
         def grads(n, lo, hi):
             return slots("w", n, lo, hi).bitcast(FP8X4), slots("s", n, lo, hi)
 
-        def turned(pair, cbs, sums_tags, turn_tags, order="qkv"):
-            cols = slice(cbs[0] * P, (cbs[-1] + 1) * P)
-            width = len(cbs) * P
-            gated = keep.tile([P, 4, width], F32, name=f"gated{pair}_{cbs[0]}")
-            if len(sums_tags) == 4:
-                sums = [psum.tile([P, width], F32, name=f"sums{pair}_{cbs[0]}_{b}", tag=tag)[:] for b, tag in enumerate(sums_tags)]
-                passes = [(b, n) for n in order for b in range(4)]
-            else:
-                banks = [psum.tile([P, 2, width], F32, name=f"sums{pair}_{cbs[0]}_{u}", tag=tag) for u, tag in enumerate(sums_tags)]
-                sums = [banks[b // 2][:, b % 2, :] for b in range(4)]
-                passes = [(b, n) for b in range(4) for n in order]
-            for b, n in passes:
-                lo = pair * PAIR + b * P
-                gw, gs = grads(n, lo, lo + P)
-                ww, ws = weights(2 * pair + b // 2, n, cols)
-                nc.tensor.matmul_mx(out=sums[b], lhsT=gw, lhsT_scale=gs, rhs=ww, rhs_scale=ws,
-                                    start=(n == order[0]), stop=(n == order[-1]))
+        def weights(e, n, lo, hi):
+            if n == "v" and e >= WHOLE:
+                return wv_late[lo // P][:, e - WHOLE, :].bitcast(FP8X4), w_scales[n][:, e, lo:hi]
+            if n != "k":
+                return w_words[n, e // 2][:, e % 2, lo:hi].bitcast(FP8X4), w_scales[n][:, e, lo:hi]
+            h, at = (0, e * K + lo) if e < WHOLE else (1 + lo // P, (e - WHOLE) * P)
+            return wk_codes[h][:, at:at + hi - lo].bitcast(FP8X4), wk_scales[h][:, at:at + hi - lo]
+
+        def turned(pair, gated, sums_tags, turn_tags):
+            width = gated.shape[2]
+            per = 4 // len(sums_tags)
+            banks = [psum.tile([P, per, width], F32, name=f"sums{pair}_{u}", tag=tag) for u, tag in enumerate(sums_tags)]
+            sums = [banks[b // per][:, b % per, :] for b in range(4)]
+            for n in "qkv":
+                for b in range(4):
+                    lo = pair * PAIR + b * P
+                    gw, gs = grads(n, lo, lo + P)
+                    ww, ws = weights(2 * pair + b // 2, n, 0, width)
+                    nc.tensor.matmul_mx(out=sums[b], lhsT=gw, lhsT_scale=gs, rhs=ww, rhs_scale=ws,
+                                        start=(n == "q" and b % per == 0), stop=(n == "v" and b % per == per - 1))
             for b in range(4):
                 nc.scalar.activation(gated[:, b, :], sums[b], COPY, scale=gate_cols[:, 4 * pair + b:4 * pair + b + 1])
-            parts = len(turn_tags) // len(cbs)
+            parts = len(turn_tags) * P // width
             blocks = 4 // parts
-            for j, cb in enumerate(cbs):
+            for cb in range(width // P):
                 for part in range(parts):
-                    turn = psum.tile([P, blocks * P], F32, name=f"turn{pair}_{cb}_{part}", tag=turn_tags[j * parts + part])
+                    turn = psum.tile([P, blocks * P], F32, name=f"turn{pair}_{cb}_{part}", tag=turn_tags[cb * parts + part])
                     for b in range(blocks):
                         nc.tensor.transpose(turn[:, b * P:(b + 1) * P],
-                                            gated[:, part * blocks + b, j * P:(j + 1) * P], identity[:])
+                                            gated[:, part * blocks + b, cb * P:(cb + 1) * P], identity[:])
                     lo = pair * PAIR + part * blocks * P
                     nc.scalar.copy(dx[cb][:, lo:lo + blocks * P], turn[:])
 
-        def direct(tags):
-            sums = {(u, cb): psum.tile([P, C], F32, name=f"direct{u}_{cb}", tag=tags[2 * cb + u])
-                    for cb in range(2) for u in range(2)}
-            early = [(u, cb, n) for cb in range(2) for u in range(2) for n in "qv"]
-            late = [(u, cb, "k") for cb in range(2) for u in range(2)]
-            for u, cb, n in early + late:
-                e = TURNED + u
-                gw, gs = grads(n, e * C, (e + 1) * C)
-                ww, ws = weights(e, n, slice(cb * P, (cb + 1) * P))
-                nc.tensor.matmul_mx(out=sums[u, cb][:], lhsT=ww, lhsT_scale=ws, rhs=gw, rhs_scale=gs,
-                                    start=(n == "q"), stop=(n == "k"))
-            for u, cb, n in late:
-                e = TURNED + u
-                nc.vector.tensor_tensor(dx[cb][:, e * C:(e + 1) * C], sums[u, cb][:], gate_last[:, u * C:(u + 1) * C], MULT)
+        def direct_pass(bank, cb, experts, e, n):
+            gw, gs = grads(n, e * C, (e + 1) * C)
+            ww, ws = weights(e, n, cb * P, (cb + 1) * P)
+            at = (e - experts[0]) * C
+            nc.tensor.matmul_mx(out=bank[:, at:at + C], lhsT=ww, lhsT_scale=ws, rhs=gw, rhs_scale=gs,
+                                start=(n == "q" and e == experts[0]), stop=(n == "k" and e == experts[-1]))
+
+        def gate_direct(bank, cb, experts):
+            lo, hi = experts[0] * C, (experts[-1] + 1) * C
+            nc.vector.tensor_tensor(dx[cb][:, lo:hi], bank[:], gate_late[:, lo - HALF:hi - HALF], MULT)
 
         gathered("s", "q", 0, S)
-        gathered("w", "q", 0, HALF)
-        gathered("w", "k", 0, HALF)
+        gathered("w", "q", 0, S)
         gathered("s", "k", 0, HALF)
+        gathered("w", "k", 0, HALF)
         gathered("w", "v", 0, HALF)
-        quantise(0, 0, 4)
-        gathered("s", "v", 0, HALF, 14336)
-        gathered("w", "q", HALF, S, 0)
-        quantise(1, 0, 2)
-        quantise(1, 2, 3)
-        gathered("s", "k", HALF, HALF + PAIR, 15360)
-        gathered("w", "k", HALF, HALF + PAIR, 5120)
-        gathered("w", "v", HALF, HALF + PAIR, 7168)
-        gathered("s", "v", HALF, HALF + PAIR, 9216)
-        gathered("s", "v", HALF + PAIR, S, 4352)
-        gathered("w", "v", HALF + PAIR, S, 9728)
-        gathered("w", "k", HALF + PAIR, S, 12160)
-        gathered("s", "k", 6 * C, 7 * C, 11776)
-        gathered("s", "k", 7 * C, 8 * C, 4096)
-        quantise(2, 0, 1)
-        turned(0, (0, 1), ("b0", "b1"), ("b2", "b3"))
-        turned(1, (0, 1), ("b4", "b5"), ("b2", "b3", "b6", "b7"))
-        turned(2, (0, 1), ("b2", "b3", "b6", "b7"), ("b0", "b1", "b4", "b5"))
-        direct(("b6", "b7", "b0", "b1"))
+        quantise(0)
+        gathered("s", "v", 0, HALF, RAW3_AT)
+        gathered("s", "v", HALF, S, 0)
+        quantise(1)
+        gathered("s", "k", HALF, LAST, 1024)
+        gathered("w", "k", HALF, LAST, 2048)
+        gathered("w", "v", HALF, LAST, 4096)
+        gathered("w", "v", LAST, S, 6144)
+        gathered("w", "k", LAST, S, 8192)
+        gathered("s", "k", LAST, LAST + C, 1536)
+        gathered("s", "k", LAST + C, S, 1792)
+        gated = [keep.tile([P, 4, K], F32, name="gated0"),
+                 share.tile([P, 4, K], F32, name="gated1", offset=GATED1_AT),
+                 share.tile([P, 4, P], F32, name="gated2", offset=GATED2_AT)]
+        turned(0, gated[0], ("b0", "b1"), ("b2", "b3"))
+        turned(1, gated[1], ("b4", "b5"), ("b2", "b3"))
+        wv_late.append(share.tile([P, E - WHOLE, P], I32, name="wv_late1", align_bytes=64, offset=GATED1_AT))
+        nc.sync.dma_start(wv_late[1][:], wv_rows[:, :, P:])
+        turned(2, gated[2], ("b2",), ("b0", "b1"))
+        wk_codes.append(share.tile([P, widths[2]], U32, name="wk_codes2", align_bytes=64, offset=GATED2_AT))
+        quantise(2)
 
-        fetch = 256
-        stores = (((0, 512), (512, T)), ((0, 512), (512, 896), (896, T)))
-        for cb in range(2):
-            first = {}
-            for lo in range(0, T, fetch):
-                first[lo] = keep.tile([P, fetch], F32, name=f"first{cb}_{lo}")
-                nc.scalar.activation(first[lo][:], dx[cb][:].indirect(pos1_sb[:, lo // LIST:(lo + fetch) // LIST]), COPY)
-            for lo, hi in stores[cb]:
+        groups = ((0, (6,), "b0"), (0, (7,), "b1"), (1, (4, 5), "b6"), (1, (6, 7), "b7"))
+        banks = [psum.tile([P, len(experts) * C], F32, name=f"direct{tag}", tag=tag) for cb, experts, tag in groups]
+        for names in ("qv", "k"):
+            for bank, (cb, experts, tag) in zip(banks, groups):
+                for n in names:
+                    for e in experts:
+                        direct_pass(bank, cb, experts, e, n)
+        for bank, (cb, experts, tag) in zip(banks, groups):
+            gate_direct(bank, cb, experts)
+
+        first = [keep.tile([P, T], F32, name=f"first{cb}") for cb in range(2)]
+
+        seen = []
+        for cb, cuts in ((0, (0, 384, 704, T)), (1, (0, 384, 768, T))):
+            for lo, hi in zip(cuts, cuts[1:]):
                 both = keep.tile([P, hi - lo], F32, name=f"both{cb}_{lo}")
-                a = lo
-                while a < hi:
-                    base = a - a % fetch
-                    b = min(hi, base + fetch)
-                    nc.vector.tensor_tensor(both[:, a - lo:b - lo], dx[cb][:].indirect(pos2_sb[:, a // LIST:b // LIST]),
-                                            first[base][:, a - base:b - base], ADD)
-                    a = b
+                nc.scalar.activation(first[cb][:, lo:hi], dx[cb][:].indirect(pos1_sb[:, lo // LIST:hi // LIST]), COPY)
+                nc.vector.tensor_tensor(both[:], dx[cb][:].indirect(pos2_sb[:, lo // LIST:hi // LIST]), first[cb][:, lo:hi], ADD)
                 nc.sync.dma_start(out[cb * P:(cb + 1) * P, lo:hi], both[:])
+                seen.append(both)

@@ -25,7 +25,6 @@ LIST = 16
 HALF = S // 2
 LAST = TURNED * C
 WIDE = 1376
-WIDEST = 4096
 WHOLE = E // 2
 RAW3_AT = 16384
 GATED1_AT = 20480
@@ -45,9 +44,8 @@ def tile_moe_qkb_kernel(
         offs_sb = keep.tile([P, S // LIST], U16, name="offs_sb")
         pos1_sb = keep.tile([P, T // LIST], U16, name="pos1_sb")
         pos2_sb = keep.tile([P, T // LIST], U16, name="pos2_sb")
-        window = {"q": WIDEST, "k": WIDE, "v": WIDE}
-        d_words = {n: keep.tile([P, window[n]], I32, name=f"d{n}_words_sb", align_bytes=64) for n in "qkv"}
-        d_scales = {n: keep.tile([P, window[n]], U8, name=f"d{n}_scales_sb", align_bytes=64) for n in "qkv"}
+        d_words = {n: keep.tile([P, WIDE if n == "q" else S], I32, name=f"d{n}_words_sb", align_bytes=64) for n in "qkv"}
+        d_scales = {n: keep.tile([P, S if n == "k" else WIDE], U8, name=f"d{n}_scales_sb", align_bytes=64) for n in "qkv"}
         w_scales = {n: keep.tile([P, E, K], U8, name=f"w{n}_scales_sb", align_bytes=64) for n in "qv"}
         w_words = {(n, pair): keep.tile([P, 2, K], I32, name=f"w{n}_words_sb{pair}", align_bytes=64)
                    for n in "qv" for pair in range(E // 2) if n == "q" or pair < WHOLE // 2}
@@ -123,9 +121,10 @@ def tile_moe_qkb_kernel(
         wk_scales = [keep.tile([P, w], U8, name=f"wk_scales{h}", align_bytes=64) for h, w in enumerate(widths)]
         for e in range(WHOLE):
             nc.scalar.copy(casts[0][:, e * K:(e + 1) * K], wk_raw[e][:].rearrange("p t c -> p c t"))
-        for cb in range(2):
-            nc.scalar.copy(casts[1 + cb][:].rearrange("p (e c) t -> p e c t", e=E - WHOLE),
-                           wk_late[:, :, :, cb * P:(cb + 1) * P].rearrange("p e t c -> p e c t"))
+        for u in range(0, E - WHOLE, 2):
+            for cb in range(2):
+                nc.scalar.copy(casts[1 + cb][:, u * P:(u + 2) * P].rearrange("p (e c) t -> p e c t", e=2),
+                               wk_late[:, u:u + 2, :, cb * P:(cb + 1) * P].rearrange("p e t c -> p e c t"))
 
         def quantise(h):
             nc.vector.quantize_mx(out=wk_codes[h][:].bitcast(FP8X4), scales=wk_scales[h][:],
@@ -193,42 +192,49 @@ def tile_moe_qkb_kernel(
             lo, hi = experts[0] * C, (experts[-1] + 1) * C
             nc.vector.tensor_tensor(dx[cb][:, lo:hi], bank[:], gate_late[:, lo - HALF:hi - HALF], MULT)
 
-        gathered("s", "q", 0, S)
-        gathered("w", "q", 0, S)
-        gathered("s", "k", 0, HALF)
-        gathered("w", "k", 0, HALF)
-        gathered("w", "v", 0, HALF)
+        gathered("s", "q", 0, HALF)
+        gathered("w", "q", 0, HALF)
+        gathered("s", "k", 0, LAST)
+        gathered("w", "k", 0, LAST)
+        gathered("w", "v", 0, LAST)
         quantise(0)
         gathered("s", "v", 0, HALF, RAW3_AT)
-        gathered("s", "v", HALF, S, 0)
         quantise(1)
-        gathered("s", "k", HALF, LAST, 1024)
-        gathered("w", "k", HALF, LAST, 2048)
-        gathered("w", "v", HALF, LAST, 4096)
-        gathered("w", "v", LAST, S, 6144)
-        gathered("w", "k", LAST, S, 8192)
-        gathered("s", "k", LAST, LAST + C, 1536)
-        gathered("s", "k", LAST + C, S, 1792)
+        gathered("s", "q", HALF, S, 0)
+        gathered("w", "q", HALF, S, 4096)
+        gathered("s", "v", HALF, S, 1024)
+        gathered("w", "v", LAST, S, 8192)
+        gathered("w", "k", LAST, S, 10240)
+        gathered("s", "k", LAST, LAST + C, 2048)
+        gathered("s", "k", LAST + C, S, 2304)
         gated = [keep.tile([P, 4, K], F32, name="gated0"),
                  share.tile([P, 4, K], F32, name="gated1", offset=GATED1_AT),
                  share.tile([P, 4, P], F32, name="gated2", offset=GATED2_AT)]
         turned(0, gated[0], ("b0", "b1"), ("b2", "b3"))
-        turned(1, gated[1], ("b4", "b5"), ("b2", "b3"))
+        turned(1, gated[1], ("b4", "b5"), ("b2", "b3", "b6", "b7"))
+        groups = ((0, (6,), "b0"), (0, (7,), "b1"), (1, (4, 5), "b6"), (1, (6, 7), "b7"))
+        banks = {}
+
+        def direct(which, names):
+            for cb, experts, tag in which:
+                if tag not in banks:
+                    banks[tag] = psum.tile([P, len(experts) * C], F32, name=f"direct{tag}", tag=tag)
+                for n in names:
+                    for e in experts:
+                        direct_pass(banks[tag], cb, experts, e, n)
+
+        direct(groups[2:], "q")
         wv_late.append(share.tile([P, E - WHOLE, P], I32, name="wv_late1", align_bytes=64, offset=GATED1_AT))
         nc.sync.dma_start(wv_late[1][:], wv_rows[:, :, P:])
         turned(2, gated[2], ("b2",), ("b0", "b1"))
         wk_codes.append(share.tile([P, widths[2]], U32, name="wk_codes2", align_bytes=64, offset=GATED2_AT))
         quantise(2)
 
-        groups = ((0, (6,), "b0"), (0, (7,), "b1"), (1, (4, 5), "b6"), (1, (6, 7), "b7"))
-        banks = [psum.tile([P, len(experts) * C], F32, name=f"direct{tag}", tag=tag) for cb, experts, tag in groups]
-        for names in ("qv", "k"):
-            for bank, (cb, experts, tag) in zip(banks, groups):
-                for n in names:
-                    for e in experts:
-                        direct_pass(bank, cb, experts, e, n)
-        for bank, (cb, experts, tag) in zip(banks, groups):
-            gate_direct(bank, cb, experts)
+        direct(groups[:2], "qv")
+        direct(groups[2:], "v")
+        direct(groups, "k")
+        for cb, experts, tag in groups:
+            gate_direct(banks[tag], cb, experts)
 
         first = [keep.tile([P, T], F32, name=f"first{cb}") for cb in range(2)]
 

@@ -45,7 +45,7 @@ def tile_moe_qkb_kernel(
         pos1_sb = keep.tile([P, T // LIST], U16, name="pos1_sb")
         pos2_sb = keep.tile([P, T // LIST], U16, name="pos2_sb")
         d_words = {n: keep.tile([P, WIDE if n == "q" else S], I32, name=f"d{n}_words_sb", align_bytes=64) for n in "qkv"}
-        d_scales = {n: keep.tile([P, S if n == "k" else WIDE], U8, name=f"d{n}_scales_sb", align_bytes=64) for n in "qkv"}
+        d_scales = {n: keep.tile([P, {"q": 2 * S, "k": S, "v": WIDE}[n]], U8, name=f"d{n}_scales_sb", align_bytes=64) for n in "qkv"}
         w_scales = {n: keep.tile([P, E, K], U8, name=f"w{n}_scales_sb", align_bytes=64) for n in "qv"}
         w_words = {(n, pair): keep.tile([P, 2, K], I32, name=f"w{n}_words_sb{pair}", align_bytes=64)
                    for n in "qv" for pair in range(E // 2) if n == "q" or pair < WHOLE // 2}
@@ -156,7 +156,7 @@ def tile_moe_qkb_kernel(
             h, at = (0, e * K + lo) if e < WHOLE else (1 + lo // P, (e - WHOLE) * P)
             return wk_codes[h][:, at:at + hi - lo].bitcast(FP8X4), wk_scales[h][:, at:at + hi - lo]
 
-        def turned(pair, gated, sums_tags, turn_tags):
+        def turned(pair, gated, sums_tags):
             width = gated.shape[2]
             per = 4 // len(sums_tags)
             banks = [psum.tile([P, per, width], F32, name=f"sums{pair}_{u}", tag=tag) for u, tag in enumerate(sums_tags)]
@@ -170,16 +170,16 @@ def tile_moe_qkb_kernel(
                                         start=(n == "q" and b % per == 0), stop=(n == "v" and b % per == per - 1))
             for b in range(4):
                 nc.scalar.activation(gated[:, b, :], sums[b], COPY, scale=gate_cols[:, 4 * pair + b:4 * pair + b + 1])
-            parts = len(turn_tags) * P // width
-            blocks = 4 // parts
-            for cb in range(width // P):
-                for part in range(parts):
-                    turn = psum.tile([P, blocks * P], F32, name=f"turn{pair}_{cb}_{part}", tag=turn_tags[cb * parts + part])
-                    for b in range(blocks):
-                        nc.tensor.transpose(turn[:, b * P:(b + 1) * P],
-                                            gated[:, part * blocks + b, cb * P:(cb + 1) * P], identity[:])
-                    lo = pair * PAIR + part * blocks * P
-                    nc.scalar.copy(dx[cb][:, lo:lo + blocks * P], turn[:])
+
+        def turn_back(pair, gated, cb, tags):
+            blocks = 4 // len(tags)
+            for part, tag in enumerate(tags):
+                turn = psum.tile([P, blocks * P], F32, name=f"turn{pair}_{cb}_{part}", tag=tag)
+                for b in range(blocks):
+                    nc.tensor.transpose(turn[:, b * P:(b + 1) * P],
+                                        gated[:, part * blocks + b, cb * P:(cb + 1) * P], identity[:])
+                lo = pair * PAIR + part * blocks * P
+                nc.scalar.copy(dx[cb][:, lo:lo + blocks * P], turn[:])
 
         def direct_pass(bank, cb, experts, e, n):
             gw, gs = grads(n, e * C, (e + 1) * C)
@@ -192,7 +192,7 @@ def tile_moe_qkb_kernel(
             lo, hi = experts[0] * C, (experts[-1] + 1) * C
             nc.vector.tensor_tensor(dx[cb][:, lo:hi], bank[:], gate_late[:, lo - HALF:hi - HALF], MULT)
 
-        gathered("s", "q", 0, HALF)
+        gathered("s", "q", 0, S)
         gathered("w", "q", 0, HALF)
         gathered("s", "k", 0, LAST)
         gathered("w", "k", 0, LAST)
@@ -200,7 +200,6 @@ def tile_moe_qkb_kernel(
         quantise(0)
         gathered("s", "v", 0, HALF, RAW3_AT)
         quantise(1)
-        gathered("s", "q", HALF, S, 0)
         gathered("w", "q", HALF, S, 4096)
         gathered("s", "v", HALF, S, 1024)
         gathered("w", "v", LAST, S, 8192)
@@ -210,8 +209,12 @@ def tile_moe_qkb_kernel(
         gated = [keep.tile([P, 4, K], F32, name="gated0"),
                  share.tile([P, 4, K], F32, name="gated1", offset=GATED1_AT),
                  share.tile([P, 4, P], F32, name="gated2", offset=GATED2_AT)]
-        turned(0, gated[0], ("b0", "b1"), ("b2", "b3"))
-        turned(1, gated[1], ("b4", "b5"), ("b2", "b3", "b6", "b7"))
+        turned(0, gated[0], ("b0", "b1"))
+        turn_back(0, gated[0], 0, ("b2",))
+        turned(1, gated[1], ("b4", "b5"))
+        turn_back(1, gated[1], 0, ("b3", "b2"))
+        turn_back(0, gated[0], 1, ("b6",))
+        turn_back(1, gated[1], 1, ("b7",))
         groups = ((0, (6,), "b0"), (0, (7,), "b1"), (1, (4, 5), "b6"), (1, (6, 7), "b7"))
         banks = {}
 
@@ -226,7 +229,8 @@ def tile_moe_qkb_kernel(
         direct(groups[2:], "q")
         wv_late.append(share.tile([P, E - WHOLE, P], I32, name="wv_late1", align_bytes=64, offset=GATED1_AT))
         nc.sync.dma_start(wv_late[1][:], wv_rows[:, :, P:])
-        turned(2, gated[2], ("b2",), ("b0", "b1"))
+        turned(2, gated[2], ("b3",))
+        turn_back(2, gated[2], 0, ("b0", "b1"))
         wk_codes.append(share.tile([P, widths[2]], U32, name="wk_codes2", align_bytes=64, offset=GATED2_AT))
         quantise(2)
 

@@ -27,8 +27,8 @@ LAST = TURNED * C
 WIDE = 1376
 WHOLE = E // 2
 RAW3_AT = 16384
-GATED1_AT = 20480
-GATED2_AT = 24576
+GATED1_AT = 24576
+GATED2_AT = 28672
 
 
 def tile_moe_qkb_kernel(
@@ -45,7 +45,7 @@ def tile_moe_qkb_kernel(
         pos1_sb = keep.tile([P, T // LIST], U16, name="pos1_sb")
         pos2_sb = keep.tile([P, T // LIST], U16, name="pos2_sb")
         d_words = {n: keep.tile([P, WIDE if n == "q" else S], I32, name=f"d{n}_words_sb", align_bytes=64) for n in "qkv"}
-        d_scales = {n: keep.tile([P, {"q": 2 * S, "k": S, "v": WIDE}[n]], U8, name=f"d{n}_scales_sb", align_bytes=64) for n in "qkv"}
+        d_scales = {n: keep.tile([P, S if n == "k" else WIDE], U8, name=f"d{n}_scales_sb", align_bytes=64) for n in "qkv"}
         w_scales = {n: keep.tile([P, E, K], U8, name=f"w{n}_scales_sb", align_bytes=64) for n in "qv"}
         w_words = {(n, pair): keep.tile([P, 2, K], I32, name=f"w{n}_words_sb{pair}", align_bytes=64)
                    for n in "qv" for pair in range(E // 2) if n == "q" or pair < WHOLE // 2}
@@ -156,18 +156,18 @@ def tile_moe_qkb_kernel(
             h, at = (0, e * K + lo) if e < WHOLE else (1 + lo // P, (e - WHOLE) * P)
             return wk_codes[h][:, at:at + hi - lo].bitcast(FP8X4), wk_scales[h][:, at:at + hi - lo]
 
-        def turned(pair, gated, sums_tags):
+        def turned(pair, gated, sums_tags, order):
             width = gated.shape[2]
             per = 4 // len(sums_tags)
             banks = [psum.tile([P, per, width], F32, name=f"sums{pair}_{u}", tag=tag) for u, tag in enumerate(sums_tags)]
             sums = [banks[b // per][:, b % per, :] for b in range(4)]
-            for n in "qkv":
+            for n in order:
                 for b in range(4):
                     lo = pair * PAIR + b * P
                     gw, gs = grads(n, lo, lo + P)
                     ww, ws = weights(2 * pair + b // 2, n, 0, width)
                     nc.tensor.matmul_mx(out=sums[b], lhsT=gw, lhsT_scale=gs, rhs=ww, rhs_scale=ws,
-                                        start=(n == "q" and b % per == 0), stop=(n == "v" and b % per == per - 1))
+                                        start=(n == order[0] and b % per == 0), stop=(n == order[-1] and b % per == per - 1))
             for b in range(4):
                 nc.scalar.activation(gated[:, b, :], sums[b], COPY, scale=gate_cols[:, 4 * pair + b:4 * pair + b + 1])
 
@@ -192,14 +192,15 @@ def tile_moe_qkb_kernel(
             lo, hi = experts[0] * C, (experts[-1] + 1) * C
             nc.vector.tensor_tensor(dx[cb][:, lo:hi], bank[:], gate_late[:, lo - HALF:hi - HALF], MULT)
 
-        gathered("s", "q", 0, S)
+        gathered("s", "q", 0, HALF)
         gathered("w", "q", 0, HALF)
         gathered("s", "k", 0, LAST)
         gathered("w", "k", 0, LAST)
-        gathered("w", "v", 0, LAST)
         quantise(0)
+        gathered("w", "v", 0, LAST, RAW3_AT + 1024)
         gathered("s", "v", 0, HALF, RAW3_AT)
         quantise(1)
+        gathered("s", "q", HALF, S, 0)
         gathered("w", "q", HALF, S, 4096)
         gathered("s", "v", HALF, S, 1024)
         gathered("w", "v", LAST, S, 8192)
@@ -209,12 +210,12 @@ def tile_moe_qkb_kernel(
         gated = [keep.tile([P, 4, K], F32, name="gated0"),
                  share.tile([P, 4, K], F32, name="gated1", offset=GATED1_AT),
                  share.tile([P, 4, P], F32, name="gated2", offset=GATED2_AT)]
-        turned(0, gated[0], ("b0", "b1"))
+        turned(0, gated[0], ("b0", "b1"), "kqv")
         turn_back(0, gated[0], 0, ("b2",))
-        turned(1, gated[1], ("b4", "b5"))
-        turn_back(1, gated[1], 0, ("b3", "b2"))
-        turn_back(0, gated[0], 1, ("b6",))
-        turn_back(1, gated[1], 1, ("b7",))
+        turn_back(0, gated[0], 1, ("b3",))
+        turned(1, gated[1], ("b4", "b5"), "kqv")
+        turn_back(1, gated[1], 0, ("b2", "b3"))
+        turn_back(1, gated[1], 1, ("b6", "b7"))
         groups = ((0, (6,), "b0"), (0, (7,), "b1"), (1, (4, 5), "b6"), (1, (6, 7), "b7"))
         banks = {}
 
@@ -229,7 +230,7 @@ def tile_moe_qkb_kernel(
         direct(groups[2:], "q")
         wv_late.append(share.tile([P, E - WHOLE, P], I32, name="wv_late1", align_bytes=64, offset=GATED1_AT))
         nc.sync.dma_start(wv_late[1][:], wv_rows[:, :, P:])
-        turned(2, gated[2], ("b3",))
+        turned(2, gated[2], ("b2",), "kqv")
         turn_back(2, gated[2], 0, ("b0", "b1"))
         wk_codes.append(share.tile([P, widths[2]], U32, name="wk_codes2", align_bytes=64, offset=GATED2_AT))
         quantise(2)

@@ -20,15 +20,20 @@ ADD = mybir.AluOpType.add
 P = 128
 S = E * C
 PAIR = 2 * C
-TURNED = E - 2
-LIST = 16
-HALF = S // 2
-LAST = TURNED * C
-WIDE = 1376
-WHOLE = E // 2
+PER_COLUMN = 16
+EARLY = E // 2
+HALF = EARLY * C
+LAST = (E - 2) * C
+TURNED_BLOCKS = LAST // P
+
+ROOM_FOR_HALF = 1376
+ROOM_FOR_LAST = 2048
+
 RAW3_AT = 16384
 GATED1_AT = 24576
 GATED2_AT = 28672
+
+CUTS = ((0, 384, 704, T), (0, 384, 768, T))
 
 
 def tile_moe_qkb_kernel(
@@ -41,20 +46,22 @@ def tile_moe_qkb_kernel(
         share = ctx.enter_context(tc.tile_pool(name="share", bufs=1))
         psum = ctx.enter_context(tc.psum_pool(name="psum", bufs=1))
 
-        offs_sb = keep.tile([P, S // LIST], U16, name="offs_sb")
-        pos1_sb = keep.tile([P, T // LIST], U16, name="pos1_sb")
-        pos2_sb = keep.tile([P, T // LIST], U16, name="pos2_sb")
-        d_words = {n: keep.tile([P, WIDE if n == "q" else S], I32, name=f"d{n}_words_sb", align_bytes=64) for n in "qkv"}
-        d_scales = {n: keep.tile([P, S if n == "k" else WIDE], U8, name=f"d{n}_scales_sb", align_bytes=64) for n in "qkv"}
+        offs_sb = keep.tile([P, S // PER_COLUMN], U16, name="offs_sb")
+        pos1_sb = keep.tile([P, T // PER_COLUMN], U16, name="pos1_sb")
+        pos2_sb = keep.tile([P, T // PER_COLUMN], U16, name="pos2_sb")
+        d_words = {n: keep.tile([P, ROOM_FOR_HALF if n == "q" else ROOM_FOR_LAST], I32, name=f"d{n}_words_sb",
+                                align_bytes=64) for n in "qkv"}
+        d_scales = {n: keep.tile([P, ROOM_FOR_LAST if n == "k" else ROOM_FOR_HALF], U8, name=f"d{n}_scales_sb",
+                                 align_bytes=64) for n in "qkv"}
         w_scales = {n: keep.tile([P, E, K], U8, name=f"w{n}_scales_sb", align_bytes=64) for n in "qv"}
         w_words = {(n, pair): keep.tile([P, 2, K], I32, name=f"w{n}_words_sb{pair}", align_bytes=64)
-                   for n in "qv" for pair in range(E // 2) if n == "q" or pair < WHOLE // 2}
-        wv_late = [keep.tile([P, E - WHOLE, P], I32, name="wv_late0", align_bytes=64)]
-        wk_raw = [share.tile([P, 4, K], F32, name=f"wk_raw{e}", offset=RAW3_AT) if e == 3
-                  else keep.tile([P, 4, K], F32, name=f"wk_raw{e}") for e in range(WHOLE)]
-        wk_late = share.tile([P, E - WHOLE, 4, K], F32, name="wk_late", offset=0)
+                   for n in "qv" for pair in range(E // 2) if n == "q" or pair < EARLY // 2}
+        wv_late = [keep.tile([P, E - EARLY, P], I32, name="wv_late0", align_bytes=64)]
+        wk_raw = [share.tile([P, 4, K], F32, name=f"wk_raw{e}", offset=RAW3_AT) if e == EARLY - 1
+                  else keep.tile([P, 4, K], F32, name=f"wk_raw{e}") for e in range(EARLY)]
+        wk_late = share.tile([P, E - EARLY, 4, K], F32, name="wk_late", offset=0)
         gate_rows = keep.tile([P, P], F32, name="gate_rows")
-        gate_cols = keep.tile([P, S // P], F32, name="gate_cols")
+        gate_cols = keep.tile([P, TURNED_BLOCKS], F32, name="gate_cols")
         gate_late = keep.tile([P, HALF], F32, name="gate_late")
         identity = keep.tile([P, P], F32, name="identity")
         dx = [keep.tile([P, S], F32, name=f"dx{cb}") for cb in range(2)]
@@ -97,42 +104,42 @@ def tile_moe_qkb_kernel(
         load_wk(2)
         load_wk(3)
         load_words("v", dv_words)
-        for e in range(WHOLE, E, 2):
-            nc.sync.dma_start(wk_late[:, e - WHOLE:e - WHOLE + 2].rearrange("p e j c -> p e (j c)"),
+        for e in range(EARLY, E, 2):
+            nc.sync.dma_start(wk_late[:, e - EARLY:e - EARLY + 2].rearrange("p e j c -> p e (j c)"),
                               wk[e:e + 2].rearrange("e (p j) c -> p e (j c)", j=4))
-        nc.sync.dma_start(gate_rows[0:S // P, :], gate[0].rearrange("(b p) -> b p", p=P))
+        nc.sync.dma_start(gate_rows[0:TURNED_BLOCKS, :], gate[0, 0:LAST].rearrange("(b p) -> b p", p=P))
         for n, words, scales in (("q", wq_words, wq_scales), ("v", wv_words, wv_scales)):
             load_w_words(n, 0, words)
             load_w_scales(n, scales)
             load_w_words(n, 1, words)
-        for pair in range(2, E // 2):
+        for pair in range(EARLY // 2, E // 2):
             load_w_words("q", pair, wq_words)
-        wv_rows = wv_words[WHOLE:].rearrange("e s p c d -> p (e s) (c d)").bitcast(I32)
+        wv_rows = wv_words[EARLY:].rearrange("e s p c d -> p (e s) (c d)").bitcast(I32)
         nc.sync.dma_start(wv_late[0][:], wv_rows[:, :, 0:P])
         nc.sync.dma_start(gate_late[:], gate[:, HALF:])
 
         gate_bank = psum.tile([P, P], F32, name="gate_bank", tag="b2")
         nc.tensor.transpose(gate_bank[:], gate_rows[:], identity[:])
-        nc.scalar.copy(gate_cols[:], gate_bank[:, 0:S // P])
+        nc.scalar.copy(gate_cols[:], gate_bank[:, 0:TURNED_BLOCKS])
 
-        widths = (WHOLE * K, WHOLE * P, WHOLE * P)
+        widths = (EARLY * K, (E - EARLY) * P, (E - EARLY) * P)
         casts = [keep.tile([P, w, 4], BF16, name=f"cast{h}", align_bytes=64) for h, w in enumerate(widths)]
         wk_codes = [keep.tile([P, w], U32, name=f"wk_codes{h}", align_bytes=64) for h, w in enumerate(widths[:2])]
         wk_scales = [keep.tile([P, w], U8, name=f"wk_scales{h}", align_bytes=64) for h, w in enumerate(widths)]
-        for e in range(WHOLE):
-            nc.scalar.copy(casts[0][:, e * K:(e + 1) * K], wk_raw[e][:].rearrange("p t c -> p c t"))
-        for u in range(0, E - WHOLE, 2):
+        for e in range(EARLY):
+            nc.scalar.copy(casts[0][:, e * K:(e + 1) * K], wk_raw[e][:].rearrange("p j c -> p c j"))
+        for u in range(0, E - EARLY, 2):
             for cb in range(2):
-                nc.scalar.copy(casts[1 + cb][:, u * P:(u + 2) * P].rearrange("p (e c) t -> p e c t", e=2),
-                               wk_late[:, u:u + 2, :, cb * P:(cb + 1) * P].rearrange("p e t c -> p e c t"))
+                nc.scalar.copy(casts[1 + cb][:, u * P:(u + 2) * P].rearrange("p (e c) j -> p e c j", e=2),
+                               wk_late[:, u:u + 2, :, cb * P:(cb + 1) * P].rearrange("p e j c -> p e c j"))
 
         def quantise(h):
             nc.vector.quantize_mx(out=wk_codes[h][:].bitcast(FP8X4), scales=wk_scales[h][:],
-                                  in_=casts[h][:].rearrange("p c t -> p (c t)"))
+                                  in_=casts[h][:].rearrange("p c j -> p (c j)"))
 
         pieces = {}
 
-        def gathered(kind, n, lo, hi, offset=None):
+        def gather(kind, n, lo, hi, offset=None):
             dtype = U32 if kind == "w" else U8
             if offset is None:
                 piece = keep.tile([P, hi - lo], dtype, name=f"g{n}{kind}{lo}", align_bytes=64)
@@ -140,114 +147,109 @@ def tile_moe_qkb_kernel(
                 piece = share.tile([P, hi - lo], dtype, name=f"g{n}{kind}{lo}", align_bytes=64, offset=offset)
             pieces.setdefault((kind, n), []).append((lo, hi, piece))
             table = d_words[n][:].bitcast(U32) if kind == "w" else d_scales[n][:]
-            nc.vector.tensor_copy(piece[:], table.indirect(offs_sb[:, lo // LIST:hi // LIST]))
+            nc.vector.tensor_copy(piece[:], table.indirect(offs_sb[:, lo // PER_COLUMN:hi // PER_COLUMN]))
 
-        def slots(kind, n, lo, hi):
+        def gathered(kind, n, lo, hi):
             return [piece[:, lo - a:hi - a] for a, b, piece in pieces[kind, n] if a <= lo and hi <= b][0]
 
         def grads(n, lo, hi):
-            return slots("w", n, lo, hi).bitcast(FP8X4), slots("s", n, lo, hi)
+            return gathered("w", n, lo, hi).bitcast(FP8X4), gathered("s", n, lo, hi)
 
         def weights(e, n, lo, hi):
-            if n == "v" and e >= WHOLE:
-                return wv_late[lo // P][:, e - WHOLE, :].bitcast(FP8X4), w_scales[n][:, e, lo:hi]
+            if n == "v" and e >= EARLY:
+                return wv_late[lo // P][:, e - EARLY, :].bitcast(FP8X4), w_scales[n][:, e, lo:hi]
             if n != "k":
                 return w_words[n, e // 2][:, e % 2, lo:hi].bitcast(FP8X4), w_scales[n][:, e, lo:hi]
-            h, at = (0, e * K + lo) if e < WHOLE else (1 + lo // P, (e - WHOLE) * P)
+            h, at = (0, e * K + lo) if e < EARLY else (1 + lo // P, (e - EARLY) * P)
             return wk_codes[h][:, at:at + hi - lo].bitcast(FP8X4), wk_scales[h][:, at:at + hi - lo]
 
-        def turned(pair, gated, sums_tags, order):
+        def multiply_turned(pair, gated, tags):
             width = gated.shape[2]
-            per = 4 // len(sums_tags)
-            banks = [psum.tile([P, per, width], F32, name=f"sums{pair}_{u}", tag=tag) for u, tag in enumerate(sums_tags)]
-            sums = [banks[b // per][:, b % per, :] for b in range(4)]
-            for n in order:
+            per_bank = 4 // len(tags)
+            banks = [psum.tile([P, per_bank, width], F32, name=f"sums{pair}_{u}", tag=tag) for u, tag in enumerate(tags)]
+            sums = [banks[b // per_bank][:, b % per_bank, :] for b in range(4)]
+            for n in "kqv":
                 for b in range(4):
                     lo = pair * PAIR + b * P
                     gw, gs = grads(n, lo, lo + P)
                     ww, ws = weights(2 * pair + b // 2, n, 0, width)
                     nc.tensor.matmul_mx(out=sums[b], lhsT=gw, lhsT_scale=gs, rhs=ww, rhs_scale=ws,
-                                        start=(n == order[0] and b % per == 0), stop=(n == order[-1] and b % per == per - 1))
+                                        start=(n == "k" and b % per_bank == 0),
+                                        stop=(n == "v" and b % per_bank == per_bank - 1))
             for b in range(4):
                 nc.scalar.activation(gated[:, b, :], sums[b], COPY, scale=gate_cols[:, 4 * pair + b:4 * pair + b + 1])
 
         def turn_back(pair, gated, cb, tags):
-            blocks = 4 // len(tags)
+            per_bank = 4 // len(tags)
             for part, tag in enumerate(tags):
-                turn = psum.tile([P, blocks * P], F32, name=f"turn{pair}_{cb}_{part}", tag=tag)
-                for b in range(blocks):
+                turn = psum.tile([P, per_bank * P], F32, name=f"turn{pair}_{cb}_{part}", tag=tag)
+                for b in range(per_bank):
                     nc.tensor.transpose(turn[:, b * P:(b + 1) * P],
-                                        gated[:, part * blocks + b, cb * P:(cb + 1) * P], identity[:])
-                lo = pair * PAIR + part * blocks * P
-                nc.scalar.copy(dx[cb][:, lo:lo + blocks * P], turn[:])
+                                        gated[:, part * per_bank + b, cb * P:(cb + 1) * P], identity[:])
+                lo = pair * PAIR + part * per_bank * P
+                nc.scalar.copy(dx[cb][:, lo:lo + per_bank * P], turn[:])
 
-        def direct_pass(bank, cb, experts, e, n):
-            gw, gs = grads(n, e * C, (e + 1) * C)
-            ww, ws = weights(e, n, cb * P, (cb + 1) * P)
-            at = (e - experts[0]) * C
-            nc.tensor.matmul_mx(out=bank[:, at:at + C], lhsT=ww, lhsT_scale=ws, rhs=gw, rhs_scale=gs,
-                                start=(n == "q" and e == experts[0]), stop=(n == "k" and e == experts[-1]))
+        direct_block0 = ((0, (6,), "b0"), (0, (7,), "b1"))
+        direct_block1 = ((1, (4, 5), "b6"), (1, (6, 7), "b7"))
+        direct_banks = {}
 
-        def gate_direct(bank, cb, experts):
-            lo, hi = experts[0] * C, (experts[-1] + 1) * C
-            nc.vector.tensor_tensor(dx[cb][:, lo:hi], bank[:], gate_late[:, lo - HALF:hi - HALF], MULT)
+        def multiply_direct(groups, tables):
+            for cb, experts, tag in groups:
+                if tag not in direct_banks:
+                    direct_banks[tag] = psum.tile([P, len(experts) * C], F32, name=f"direct{tag}", tag=tag)
+                for n in tables:
+                    for e in experts:
+                        gw, gs = grads(n, e * C, (e + 1) * C)
+                        ww, ws = weights(e, n, cb * P, (cb + 1) * P)
+                        at = (e - experts[0]) * C
+                        nc.tensor.matmul_mx(out=direct_banks[tag][:, at:at + C], lhsT=ww, lhsT_scale=ws,
+                                            rhs=gw, rhs_scale=gs, start=(n == "q" and e == experts[0]),
+                                            stop=(n == "k" and e == experts[-1]))
 
-        gathered("s", "q", 0, HALF)
-        gathered("w", "q", 0, HALF)
-        gathered("s", "k", 0, LAST)
-        gathered("w", "k", 0, LAST)
+        gather("s", "q", 0, HALF)
+        gather("w", "q", 0, HALF)
+        gather("s", "k", 0, LAST)
+        gather("w", "k", 0, LAST)
         quantise(0)
-        gathered("w", "v", 0, LAST, RAW3_AT + 1024)
-        gathered("s", "v", 0, HALF, RAW3_AT)
+        gather("w", "v", 0, LAST, RAW3_AT + HALF)
+        gather("s", "v", 0, HALF, RAW3_AT)
         quantise(1)
-        gathered("s", "q", HALF, S, 0)
-        gathered("w", "q", HALF, S, 4096)
-        gathered("s", "v", HALF, S, 1024)
-        gathered("w", "v", LAST, S, 8192)
-        gathered("w", "k", LAST, S, 10240)
-        gathered("s", "k", LAST, LAST + C, 2048)
-        gathered("s", "k", LAST + C, S, 2304)
+        gather("s", "q", HALF, S, 0)
+        gather("w", "q", HALF, S, 4096)
+        gather("s", "v", HALF, S, HALF)
+        gather("w", "v", LAST, S, 4096 + 4 * HALF)
+        gather("w", "k", LAST, S, 4096 + 4 * HALF + 4 * PAIR)
+        gather("s", "k", LAST, LAST + C, 2 * HALF)
+        gather("s", "k", LAST + C, S, 2 * HALF + C)
+
         gated = [keep.tile([P, 4, K], F32, name="gated0"),
                  share.tile([P, 4, K], F32, name="gated1", offset=GATED1_AT),
                  share.tile([P, 4, P], F32, name="gated2", offset=GATED2_AT)]
-        turned(0, gated[0], ("b0", "b1"), "kqv")
+        multiply_turned(0, gated[0], ("b0", "b1"))
         turn_back(0, gated[0], 0, ("b2",))
         turn_back(0, gated[0], 1, ("b3",))
-        turned(1, gated[1], ("b4", "b5"), "kqv")
+        multiply_turned(1, gated[1], ("b4", "b5"))
         turn_back(1, gated[1], 0, ("b2", "b3"))
         turn_back(1, gated[1], 1, ("b6", "b7"))
-        groups = ((0, (6,), "b0"), (0, (7,), "b1"), (1, (4, 5), "b6"), (1, (6, 7), "b7"))
-        banks = {}
-
-        def direct(which, names):
-            for cb, experts, tag in which:
-                if tag not in banks:
-                    banks[tag] = psum.tile([P, len(experts) * C], F32, name=f"direct{tag}", tag=tag)
-                for n in names:
-                    for e in experts:
-                        direct_pass(banks[tag], cb, experts, e, n)
-
-        direct(groups[2:], "q")
-        wv_late.append(share.tile([P, E - WHOLE, P], I32, name="wv_late1", align_bytes=64, offset=GATED1_AT))
+        multiply_direct(direct_block1, "q")
+        wv_late.append(share.tile([P, E - EARLY, P], I32, name="wv_late1", align_bytes=64, offset=GATED1_AT))
         nc.sync.dma_start(wv_late[1][:], wv_rows[:, :, P:])
-        turned(2, gated[2], ("b2",), "kqv")
+        multiply_turned(2, gated[2], ("b2",))
         turn_back(2, gated[2], 0, ("b0", "b1"))
         wk_codes.append(share.tile([P, widths[2]], U32, name="wk_codes2", align_bytes=64, offset=GATED2_AT))
         quantise(2)
-
-        direct(groups[:2], "qv")
-        direct(groups[2:], "v")
-        direct(groups, "k")
-        for cb, experts, tag in groups:
-            gate_direct(banks[tag], cb, experts)
+        multiply_direct(direct_block0, "qv")
+        multiply_direct(direct_block1, "v")
+        multiply_direct(direct_block0 + direct_block1, "k")
+        for cb, experts, tag in direct_block0 + direct_block1:
+            lo, hi = experts[0] * C, (experts[-1] + 1) * C
+            nc.vector.tensor_tensor(dx[cb][:, lo:hi], direct_banks[tag][:], gate_late[:, lo - HALF:hi - HALF], MULT)
 
         first = [keep.tile([P, T], F32, name=f"first{cb}") for cb in range(2)]
-
-        seen = []
-        for cb, cuts in ((0, (0, 384, 704, T)), (1, (0, 384, 768, T))):
+        for cb, cuts in enumerate(CUTS):
             for lo, hi in zip(cuts, cuts[1:]):
+                entries = slice(lo // PER_COLUMN, hi // PER_COLUMN)
                 both = keep.tile([P, hi - lo], F32, name=f"both{cb}_{lo}")
-                nc.scalar.activation(first[cb][:, lo:hi], dx[cb][:].indirect(pos1_sb[:, lo // LIST:hi // LIST]), COPY)
-                nc.vector.tensor_tensor(both[:], dx[cb][:].indirect(pos2_sb[:, lo // LIST:hi // LIST]), first[cb][:, lo:hi], ADD)
+                nc.scalar.activation(first[cb][:, lo:hi], dx[cb][:].indirect(pos1_sb[:, entries]), COPY)
+                nc.vector.tensor_tensor(both[:], dx[cb][:].indirect(pos2_sb[:, entries]), first[cb][:, lo:hi], ADD)
                 nc.sync.dma_start(out[cb * P:(cb + 1) * P, lo:hi], both[:])
-                seen.append(both)

@@ -66,8 +66,10 @@ def tile_moe_qkb_kernel(
         identity = keep.tile([P, P], F32, name="identity")
         dx = [keep.tile([P, S], F32, name=f"dx{cb}") for cb in range(2)]
 
-        nc.gpsimd.memset(d_scales["q"][:, :T].bitcast(I32), 0)
-        for n in "kv":
+        dq_rows = keep.tile([P, ROOM_FOR_HALF], U8, name="dq_rows", align_bytes=64)
+        for lo, hi in ((0, 16), (32, 64), (64, P)):
+            nc.gpsimd.memset(dq_rows[lo:hi, :T].bitcast(I32), 0)
+        for n in "kvq":
             nc.vector.memset(d_scales[n][:, :T].bitcast(I32), 0)
         nc.gpsimd.memset(gate_rows[:], 0.0)
         make_identity(nc, identity[:])
@@ -92,9 +94,7 @@ def tile_moe_qkb_kernel(
             nc.sync.dma_start(w_words[n, pair][:], two)
 
         nc.sync.dma_start(offs_sb[:], offs)
-        nc.sync.dma_start(pos1_sb[:], pos1)
-        nc.sync.dma_start(pos2_sb[:], pos2)
-        load_scales("q", dq_scales)
+        nc.sync.dma_start(dq_rows[16:32, :T].bitcast(I32), dq_scales[0].bitcast(I32))
         load_words("q", dq_words)
         load_wk(0)
         load_scales("k", dk_scales)
@@ -107,7 +107,8 @@ def tile_moe_qkb_kernel(
         for e in range(EARLY, E, 2):
             nc.sync.dma_start(wk_late[:, e - EARLY:e - EARLY + 2].rearrange("p e j c -> p e (j c)"),
                               wk[e:e + 2].rearrange("e (p j) c -> p e (j c)", j=4))
-        nc.sync.dma_start(gate_rows[0:TURNED_BLOCKS, :], gate[0, 0:LAST].rearrange("(b p) -> b p", p=P))
+        load_scales("q", dq_scales)
+        nc.gpsimd.dma_start(gate_rows[0:TURNED_BLOCKS, :], gate[0, 0:LAST].rearrange("(b p) -> b p", p=P))
         for n, words, scales in (("q", wq_words, wq_scales), ("v", wv_words, wv_scales)):
             load_w_words(n, 0, words)
             load_w_scales(n, scales)
@@ -117,6 +118,8 @@ def tile_moe_qkb_kernel(
         wv_rows = wv_words[EARLY:].rearrange("e s p c d -> p (e s) (c d)").bitcast(I32)
         nc.sync.dma_start(wv_late[0][:], wv_rows[:, :, 0:P])
         nc.sync.dma_start(gate_late[:], gate[:, HALF:])
+        nc.sync.dma_start(pos1_sb[:], pos1)
+        nc.sync.dma_start(pos2_sb[:], pos2)
 
         gate_bank = psum.tile([P, P], F32, name="gate_bank", tag="b2")
         nc.tensor.transpose(gate_bank[:], gate_rows[:], identity[:])
@@ -206,7 +209,13 @@ def tile_moe_qkb_kernel(
                                             rhs=gw, rhs_scale=gs, start=(n == "q" and e == experts[0]),
                                             stop=(n == "k" and e == experts[-1]))
 
-        gather("s", "q", 0, HALF)
+        as_gathered = keep.tile([P, HALF], U8, name="gqs_rows", align_bytes=64)
+        nc.vector.tensor_copy(as_gathered[:], dq_rows[:].indirect(offs_sb[:, 0:HALF // PER_COLUMN]))
+        dealt = keep.tile([P, HALF], U8, name="gqs_dealt", align_bytes=64)
+        for quadrant in range(4):
+            row = 16 + 4 * quadrant
+            nc.gpsimd.dma_start(dealt[32 * quadrant:32 * quadrant + 4, :].bitcast(I32), as_gathered[row:row + 4, :].bitcast(I32))
+        pieces["s", "q"] = [(0, HALF, dealt)]
         gather("w", "q", 0, HALF)
         gather("s", "k", 0, LAST)
         gather("w", "k", 0, LAST)

@@ -1,7 +1,6 @@
 from contextlib import ExitStack
 
 import concourse.mybir as mybir
-from concourse.masks import make_identity
 
 K, T, E, C, N = 256, 1024, 8, 256, 512
 FLOPS = 2 * 3 * N * K * E * C
@@ -24,16 +23,16 @@ PER_COLUMN = 16
 EARLY = E // 2
 HALF = EARLY * C
 LAST = (E - 2) * C
-TURNED_BLOCKS = LAST // P
+ROWS_AT = P - 16
 
 ROOM_FOR_HALF = 1376
-ROOM_FOR_LAST = 2048
+ROOM_FOR_ALL = 4096
 
-RAW3_AT = 16384
-GATED1_AT = 24576
-GATED2_AT = 28672
+RAW3_AT = 4096
+LATE_AT = 12288
 
-CUTS = ((0, 384, 704, T), (0, 384, 768, T))
+LEAD = 192
+CUTS = ((LEAD, 608, T), (0, 384, 768, T))
 
 
 def tile_moe_qkb_kernel(
@@ -49,30 +48,21 @@ def tile_moe_qkb_kernel(
         offs_sb = keep.tile([P, S // PER_COLUMN], U16, name="offs_sb")
         pos1_sb = keep.tile([P, T // PER_COLUMN], U16, name="pos1_sb")
         pos2_sb = keep.tile([P, T // PER_COLUMN], U16, name="pos2_sb")
-        d_words = {n: keep.tile([P, ROOM_FOR_HALF if n == "q" else ROOM_FOR_LAST], I32, name=f"d{n}_words_sb",
+        d_words = {n: keep.tile([P, ROOM_FOR_ALL if n == "q" else ROOM_FOR_HALF], I32, name=f"d{n}_words_sb",
                                 align_bytes=64) for n in "qkv"}
-        d_scales = {n: keep.tile([P, ROOM_FOR_LAST if n == "k" else ROOM_FOR_HALF], U8, name=f"d{n}_scales_sb",
+        d_scales = {n: keep.tile([P, ROOM_FOR_HALF if n == "k" else ROOM_FOR_ALL], U8, name=f"d{n}_scales_sb",
                                  align_bytes=64) for n in "qkv"}
         w_scales = {n: keep.tile([P, E, K], U8, name=f"w{n}_scales_sb", align_bytes=64) for n in "qv"}
-        w_words = {(n, pair): keep.tile([P, 2, K], I32, name=f"w{n}_words_sb{pair}", align_bytes=64)
-                   for n in "qv" for pair in range(E // 2) if n == "q" or pair < EARLY // 2}
-        wv_late = [keep.tile([P, E - EARLY, P], I32, name="wv_late0", align_bytes=64)]
+        w_words = {n: keep.tile([P, E, K], I32, name=f"w{n}_words_sb", align_bytes=64) for n in "qv"}
         wk_raw = [share.tile([P, 4, K], F32, name=f"wk_raw{e}", offset=RAW3_AT) if e == EARLY - 1
                   else keep.tile([P, 4, K], F32, name=f"wk_raw{e}") for e in range(EARLY)]
-        wk_late = share.tile([P, E - EARLY, 4, K], F32, name="wk_late", offset=0)
-        gate_rows = keep.tile([P, P], F32, name="gate_rows")
-        gate_cols = keep.tile([P, TURNED_BLOCKS], F32, name="gate_cols")
-        gate_late = keep.tile([P, HALF], F32, name="gate_late")
-        identity = keep.tile([P, P], F32, name="identity")
+        wk_late = share.tile([P, E - EARLY, 4, K], F32, name="wk_late", offset=LATE_AT)
+        gate_sb = keep.tile([P, S], F32, name="gate_sb")
         dx = [keep.tile([P, S], F32, name=f"dx{cb}") for cb in range(2)]
 
-        dq_rows = keep.tile([P, ROOM_FOR_HALF], U8, name="dq_rows", align_bytes=64)
-        for lo, hi in ((0, 16), (32, 64), (64, P)):
-            nc.gpsimd.memset(dq_rows[lo:hi, :T].bitcast(I32), 0)
-        for n in "kvq":
+        nc.gpsimd.memset(d_scales["q"][0:ROWS_AT, :T].bitcast(I32), 0)
+        for n in "vk":
             nc.vector.memset(d_scales[n][:, :T].bitcast(I32), 0)
-        nc.gpsimd.memset(gate_rows[:], 0.0)
-        make_identity(nc, identity[:])
 
         def load_words(n, src):
             nc.sync.dma_start(d_words[n][:, :T], src[0].rearrange("p t d -> p (t d)").bitcast(I32))
@@ -84,57 +74,45 @@ def tile_moe_qkb_kernel(
         def load_wk(e):
             nc.sync.dma_start(wk_raw[e][:], wk[e].rearrange("(p j) c -> p j c", j=4))
 
-        def load_w_scales(n, src):
-            rows = src.rearrange("e s b c -> (s b) e c").bitcast(I32)
+        def load_weights(n, words, scales):
+            nc.sync.dma_start(w_words[n][:], words.rearrange("e s p c d -> p (e s) (c d)").bitcast(I32))
+            rows = scales.rearrange("e s b c -> (s b) e c").bitcast(I32)
             for r in range(4):
                 nc.sync.dma_start(w_scales[n][r:P:32, :, :].bitcast(I32), rows[r:16:4, :, :])
 
-        def load_w_words(n, pair, src):
-            two = src[2 * pair:2 * pair + 2].rearrange("e s p c d -> p (e s) (c d)").bitcast(I32)
-            nc.sync.dma_start(w_words[n, pair][:], two)
-
         nc.sync.dma_start(offs_sb[:], offs)
-        nc.sync.dma_start(dq_rows[16:32, :T].bitcast(I32), dq_scales[0].bitcast(I32))
+        nc.sync.dma_start(d_scales["q"][ROWS_AT:, :T].bitcast(I32), dq_scales[0].bitcast(I32))
         load_words("q", dq_words)
         load_wk(0)
-        load_scales("k", dk_scales)
-        load_wk(1)
-        load_words("k", dk_words)
         load_scales("v", dv_scales)
-        load_wk(2)
-        load_wk(3)
+        for e in range(1, EARLY):
+            load_wk(e)
         load_words("v", dv_words)
+        load_words("k", dk_words)
+        load_scales("k", dk_scales)
         for e in range(EARLY, E, 2):
             nc.sync.dma_start(wk_late[:, e - EARLY:e - EARLY + 2].rearrange("p e j c -> p e (j c)"),
                               wk[e:e + 2].rearrange("e (p j) c -> p e (j c)", j=4))
-        load_scales("q", dq_scales)
-        nc.gpsimd.dma_start(gate_rows[0:TURNED_BLOCKS, :], gate[0, 0:LAST].rearrange("(b p) -> b p", p=P))
-        for n, words, scales in (("q", wq_words, wq_scales), ("v", wv_words, wv_scales)):
-            load_w_words(n, 0, words)
-            load_w_scales(n, scales)
-            load_w_words(n, 1, words)
-        for pair in range(EARLY // 2, E // 2):
-            load_w_words("q", pair, wq_words)
-        wv_rows = wv_words[EARLY:].rearrange("e s p c d -> p (e s) (c d)").bitcast(I32)
-        nc.sync.dma_start(wv_late[0][:], wv_rows[:, :, 0:P])
-        nc.sync.dma_start(gate_late[:], gate[:, HALF:])
+        as_gathered = keep.tile([P, S], U8, name="gqs_rows", align_bytes=64)
+        nc.vector.tensor_copy(as_gathered[:], d_scales["q"][:].indirect(offs_sb[:]))
+        dealt = keep.tile([P, S], U8, name="gqs_dealt", align_bytes=64)
+        for quadrant in range(4):
+            row = ROWS_AT + 4 * quadrant
+            nc.sync.dma_start(dealt[32 * quadrant:32 * quadrant + 4, :].bitcast(I32),
+                              as_gathered[row:row + 4, :].bitcast(I32))
+        load_weights("q", wq_words, wq_scales)
+        load_weights("v", wv_words, wv_scales)
+        nc.sync.dma_start(gate_sb[:], gate)
         nc.sync.dma_start(pos1_sb[:], pos1)
         nc.sync.dma_start(pos2_sb[:], pos2)
 
-        gate_bank = psum.tile([P, P], F32, name="gate_bank", tag="b2")
-        nc.tensor.transpose(gate_bank[:], gate_rows[:], identity[:])
-        nc.scalar.copy(gate_cols[:], gate_bank[:, 0:TURNED_BLOCKS])
-
-        widths = (EARLY * K, (E - EARLY) * P, (E - EARLY) * P)
-        casts = [keep.tile([P, w, 4], BF16, name=f"cast{h}", align_bytes=64) for h, w in enumerate(widths)]
-        wk_codes = [keep.tile([P, w], U32, name=f"wk_codes{h}", align_bytes=64) for h, w in enumerate(widths[:2])]
-        wk_scales = [keep.tile([P, w], U8, name=f"wk_scales{h}", align_bytes=64) for h, w in enumerate(widths)]
-        for e in range(EARLY):
-            nc.scalar.copy(casts[0][:, e * K:(e + 1) * K], wk_raw[e][:].rearrange("p j c -> p c j"))
-        for u in range(0, E - EARLY, 2):
-            for cb in range(2):
-                nc.scalar.copy(casts[1 + cb][:, u * P:(u + 2) * P].rearrange("p (e c) j -> p e c j", e=2),
-                               wk_late[:, u:u + 2, :, cb * P:(cb + 1) * P].rearrange("p e j c -> p e c j"))
+        casts = [keep.tile([P, EARLY * K, 4], BF16, name=f"cast{h}", align_bytes=64) for h in range(2)]
+        wk_codes = [keep.tile([P, EARLY * K], U32, name=f"wk_codes{h}", align_bytes=64) for h in range(2)]
+        wk_scales = [keep.tile([P, EARLY * K], U8, name=f"wk_scales{h}", align_bytes=64) for h in range(2)]
+        for e in range(E):
+            raw = wk_raw[e][:] if e < EARLY else wk_late[:, e - EARLY]
+            at = e % EARLY * K
+            nc.scalar.copy(casts[e // EARLY][:, at:at + K], raw.rearrange("p j c -> p c j"))
 
         def quantise(h):
             nc.vector.quantize_mx(out=wk_codes[h][:].bitcast(FP8X4), scales=wk_scales[h][:],
@@ -155,110 +133,89 @@ def tile_moe_qkb_kernel(
         def gathered(kind, n, lo, hi):
             return [piece[:, lo - a:hi - a] for a, b, piece in pieces[kind, n] if a <= lo and hi <= b][0]
 
-        def grads(n, lo, hi):
-            return gathered("w", n, lo, hi).bitcast(FP8X4), gathered("s", n, lo, hi)
-
-        def weights(e, n, lo, hi):
-            if n == "v" and e >= EARLY:
-                return wv_late[lo // P][:, e - EARLY, :].bitcast(FP8X4), w_scales[n][:, e, lo:hi]
+        def weights(e, n, cb):
+            lo, hi = cb * P, (cb + 1) * P
             if n != "k":
-                return w_words[n, e // 2][:, e % 2, lo:hi].bitcast(FP8X4), w_scales[n][:, e, lo:hi]
-            h, at = (0, e * K + lo) if e < EARLY else (1 + lo // P, (e - EARLY) * P)
-            return wk_codes[h][:, at:at + hi - lo].bitcast(FP8X4), wk_scales[h][:, at:at + hi - lo]
+                return w_words[n][:, e, lo:hi].bitcast(FP8X4), w_scales[n][:, e, lo:hi]
+            h, at = e // EARLY, e % EARLY * K
+            return wk_codes[h][:, at + lo:at + hi].bitcast(FP8X4), wk_scales[h][:, at + lo:at + hi]
 
-        def multiply_turned(pair, gated, tags):
-            width = gated.shape[2]
-            per_bank = 4 // len(tags)
-            banks = [psum.tile([P, per_bank, width], F32, name=f"sums{pair}_{u}", tag=tag) for u, tag in enumerate(tags)]
-            sums = [banks[b // per_bank][:, b % per_bank, :] for b in range(4)]
-            for n in "kqv":
-                for b in range(4):
-                    lo = pair * PAIR + b * P
-                    gw, gs = grads(n, lo, lo + P)
-                    ww, ws = weights(2 * pair + b // 2, n, 0, width)
-                    nc.tensor.matmul_mx(out=sums[b], lhsT=gw, lhsT_scale=gs, rhs=ww, rhs_scale=ws,
-                                        start=(n == "k" and b % per_bank == 0),
-                                        stop=(n == "v" and b % per_bank == per_bank - 1))
-            for b in range(4):
-                nc.scalar.activation(gated[:, b, :], sums[b], COPY, scale=gate_cols[:, 4 * pair + b:4 * pair + b + 1])
-
-        def turn_back(pair, gated, cb, tags):
-            per_bank = 4 // len(tags)
-            for part, tag in enumerate(tags):
-                turn = psum.tile([P, per_bank * P], F32, name=f"turn{pair}_{cb}_{part}", tag=tag)
-                for b in range(per_bank):
-                    nc.tensor.transpose(turn[:, b * P:(b + 1) * P],
-                                        gated[:, part * per_bank + b, cb * P:(cb + 1) * P], identity[:])
-                lo = pair * PAIR + part * per_bank * P
-                nc.scalar.copy(dx[cb][:, lo:lo + per_bank * P], turn[:])
-
-        direct_block0 = ((0, (6,), "b0"), (0, (7,), "b1"))
-        direct_block1 = ((1, (4, 5), "b6"), (1, (6, 7), "b7"))
-        direct_banks = {}
-
-        def multiply_direct(groups, tables):
-            for cb, experts, tag in groups:
-                if tag not in direct_banks:
-                    direct_banks[tag] = psum.tile([P, len(experts) * C], F32, name=f"direct{tag}", tag=tag)
-                for n in tables:
-                    for e in experts:
-                        gw, gs = grads(n, e * C, (e + 1) * C)
-                        ww, ws = weights(e, n, cb * P, (cb + 1) * P)
-                        at = (e - experts[0]) * C
-                        nc.tensor.matmul_mx(out=direct_banks[tag][:, at:at + C], lhsT=ww, lhsT_scale=ws,
-                                            rhs=gw, rhs_scale=gs, start=(n == "q" and e == experts[0]),
-                                            stop=(n == "k" and e == experts[-1]))
-
-        as_gathered = keep.tile([P, HALF], U8, name="gqs_rows", align_bytes=64)
-        nc.vector.tensor_copy(as_gathered[:], dq_rows[:].indirect(offs_sb[:, 0:HALF // PER_COLUMN]))
-        dealt = keep.tile([P, HALF], U8, name="gqs_dealt", align_bytes=64)
-        for quadrant in range(4):
-            row = 16 + 4 * quadrant
-            nc.gpsimd.dma_start(dealt[32 * quadrant:32 * quadrant + 4, :].bitcast(I32), as_gathered[row:row + 4, :].bitcast(I32))
-        pieces["s", "q"] = [(0, HALF, dealt)]
-        gather("w", "q", 0, HALF)
-        gather("s", "k", 0, LAST)
-        gather("w", "k", 0, LAST)
+        pieces["s", "q"] = [(0, S, dealt)]
+        gather("w", "q", 0, S)
+        gather("s", "v", 0, S)
         quantise(0)
-        gather("w", "v", 0, LAST, RAW3_AT + HALF)
-        gather("s", "v", 0, HALF, RAW3_AT)
+        gather("w", "v", 0, HALF, RAW3_AT + 64 - 4 * HALF)
+        gather("w", "k", 0, HALF, RAW3_AT + 64 + HALF)
+        gather("s", "k", 0, HALF, RAW3_AT + 64)
         quantise(1)
-        gather("s", "q", HALF, S, 0)
-        gather("w", "q", HALF, S, 4096)
-        gather("s", "v", HALF, S, HALF)
-        gather("w", "v", LAST, S, 4096 + 4 * HALF)
-        gather("w", "k", LAST, S, 4096 + 4 * HALF + 4 * PAIR)
-        gather("s", "k", LAST, LAST + C, 2 * HALF)
-        gather("s", "k", LAST + C, S, 2 * HALF + C)
+        gather("w", "v", HALF, S, LATE_AT)
+        gather("w", "k", HALF, LAST, LATE_AT + 4096)
+        gather("s", "k", HALF, LAST, LATE_AT + 8192)
+        gather("w", "k", LAST, S, LATE_AT + 6144)
+        gather("s", "k", LAST, LAST + C, LATE_AT + 8192 + PAIR)
+        gather("s", "k", LAST + C, S, LATE_AT + 8192 + PAIR + C)
 
-        gated = [keep.tile([P, 4, K], F32, name="gated0"),
-                 share.tile([P, 4, K], F32, name="gated1", offset=GATED1_AT),
-                 share.tile([P, 4, P], F32, name="gated2", offset=GATED2_AT)]
-        multiply_turned(0, gated[0], ("b0", "b1"))
-        turn_back(0, gated[0], 0, ("b2",))
-        turn_back(0, gated[0], 1, ("b3",))
-        multiply_turned(1, gated[1], ("b4", "b5"))
-        turn_back(1, gated[1], 0, ("b2", "b3"))
-        turn_back(1, gated[1], 1, ("b6", "b7"))
-        multiply_direct(direct_block1, "q")
-        wv_late.append(share.tile([P, E - EARLY, P], I32, name="wv_late1", align_bytes=64, offset=GATED1_AT))
-        nc.sync.dma_start(wv_late[1][:], wv_rows[:, :, P:])
-        multiply_turned(2, gated[2], ("b2",))
-        turn_back(2, gated[2], 0, ("b0", "b1"))
-        wk_codes.append(share.tile([P, widths[2]], U32, name="wk_codes2", align_bytes=64, offset=GATED2_AT))
-        quantise(2)
-        multiply_direct(direct_block0, "qv")
-        multiply_direct(direct_block1, "v")
-        multiply_direct(direct_block0 + direct_block1, "k")
-        for cb, experts, tag in direct_block0 + direct_block1:
-            lo, hi = experts[0] * C, (experts[-1] + 1) * C
-            nc.vector.tensor_tensor(dx[cb][:, lo:hi], direct_banks[tag][:], gate_late[:, lo - HALF:hi - HALF], MULT)
+        groups = [(f"b{2 * cb + pair}", ((2 * pair, cb), (2 * pair + 1, cb))) for cb in range(2) for pair in range(2)]
+        groups += [("b4", ((4, 0), (5, 0))), ("b5", ((4, 1), (5, 1))), ("b6", ((6, 0), (6, 1))), ("b7", ((7, 0),))]
+        last_group = ("b0", ((7, 1),))
+        banks = {}
+
+        def multiply(group, tables):
+            tag, sums = group
+            if sums not in banks:
+                banks[sums] = psum.tile([P, len(sums) * C], F32, name=f"sums{sums[0][0]}_{sums[0][1]}", tag=tag)
+            for n in tables:
+                for u, (e, cb) in enumerate(sums):
+                    ww, ws = weights(e, n, cb)
+                    nc.tensor.matmul_mx(out=banks[sums][:, u * C:(u + 1) * C], lhsT=ww, lhsT_scale=ws,
+                                        rhs=gathered("w", n, e * C, (e + 1) * C).bitcast(FP8X4),
+                                        rhs_scale=gathered("s", n, e * C, (e + 1) * C),
+                                        start=(n == "q" and u == 0), stop=(n == "k" and u == len(sums) - 1))
+
+        def gate_on_gpsimd(group, offset=None):
+            sums = group[1]
+            e, cb = sums[0]
+            if offset is None:
+                plain = keep.tile([P, PAIR], F32, name=f"plain{e}_{cb}")
+            else:
+                plain = share.tile([P, PAIR], F32, name=f"plain{e}_{cb}", offset=offset)
+            nc.scalar.copy(plain[:], banks[sums][:])
+            nc.gpsimd.tensor_tensor(dx[cb][:, e * C:e * C + PAIR], plain[:], gate_sb[:, e * C:e * C + PAIR], MULT)
+
+        def gate_on_vector(group):
+            sums = group[1]
+            for u, (e, cb) in enumerate(sums):
+                nc.vector.tensor_tensor(dx[cb][:, e * C:(e + 1) * C], banks[sums][:, u * C:(u + 1) * C],
+                                        gate_sb[:, e * C:(e + 1) * C], MULT)
+
+        for group in groups:
+            multiply(group, "q")
+        for group in groups[:4]:
+            multiply(group, "v")
+        for u, group in enumerate(groups[:4]):
+            multiply(group, "k")
+            gate_on_gpsimd(group, LATE_AT + 9216 + 2048 * u)
+        multiply(last_group, "q")
+        for group in groups[4:] + [last_group]:
+            multiply(group, "v")
+        for group in groups[4:6]:
+            multiply(group, "k")
+            gate_on_gpsimd(group)
+        for group in groups[6:] + [last_group]:
+            multiply(group, "k")
+            gate_on_vector(group)
 
         first = [keep.tile([P, T], F32, name=f"first{cb}") for cb in range(2)]
+        own = keep.tile([P, LEAD], F32, name="own")
+        opening = keep.tile([P, CUTS[0][1]], F32, name="opening")
+        nc.vector.tensor_copy(own[:], dx[0][:].indirect(pos1_sb[:, 0:LEAD // PER_COLUMN]))
+        nc.vector.tensor_tensor(opening[:, :LEAD], dx[0][:].indirect(pos2_sb[:, 0:LEAD // PER_COLUMN]), own[:], ADD)
         for cb, cuts in enumerate(CUTS):
             for lo, hi in zip(cuts, cuts[1:]):
                 entries = slice(lo // PER_COLUMN, hi // PER_COLUMN)
-                both = keep.tile([P, hi - lo], F32, name=f"both{cb}_{lo}")
+                opens = cb == 0 and lo == LEAD
+                both = opening if opens else keep.tile([P, hi - lo], F32, name=f"both{cb}_{lo}")
                 nc.scalar.activation(first[cb][:, lo:hi], dx[cb][:].indirect(pos1_sb[:, entries]), COPY)
-                nc.vector.tensor_tensor(both[:], dx[cb][:].indirect(pos2_sb[:, entries]), first[cb][:, lo:hi], ADD)
-                nc.sync.dma_start(out[cb * P:(cb + 1) * P, lo:hi], both[:])
+                nc.vector.tensor_tensor(both[:, LEAD:] if opens else both[:], dx[cb][:].indirect(pos2_sb[:, entries]),
+                                        first[cb][:, lo:hi], ADD)
+                nc.sync.dma_start(out[cb * P:(cb + 1) * P, (0 if opens else lo):hi], both[:])

@@ -32,7 +32,7 @@ RAW3_AT = 4096
 LATE_AT = 12288
 
 LEAD = 192
-CUTS = ((LEAD, 608, T), (0, 384, 768, T))
+CUTS = ((LEAD, 608, T), (0, 448, 864, T))
 
 
 def tile_moe_qkb_kernel(
@@ -90,9 +90,8 @@ def tile_moe_qkb_kernel(
         load_words("v", dv_words)
         load_words("k", dk_words)
         load_scales("k", dk_scales)
-        for e in range(EARLY, E, 2):
-            nc.sync.dma_start(wk_late[:, e - EARLY:e - EARLY + 2].rearrange("p e j c -> p e (j c)"),
-                              wk[e:e + 2].rearrange("e (p j) c -> p e (j c)", j=4))
+        nc.sync.dma_start(wk_late[:].rearrange("p e j c -> p e (j c)"),
+                          wk[EARLY:].rearrange("e (p j) c -> p e (j c)", j=4))
         as_gathered = keep.tile([P, S], U8, name="gqs_rows", align_bytes=64)
         nc.vector.tensor_copy(as_gathered[:], d_scales["q"][:].indirect(offs_sb[:]))
         dealt = keep.tile([P, S], U8, name="gqs_dealt", align_bytes=64)
@@ -156,21 +155,23 @@ def tile_moe_qkb_kernel(
         gather("s", "k", LAST + C, S, LATE_AT + 8192 + PAIR + C)
 
         groups = [(f"b{2 * cb + pair}", ((2 * pair, cb), (2 * pair + 1, cb))) for cb in range(2) for pair in range(2)]
-        groups += [("b4", ((4, 0), (5, 0))), ("b5", ((4, 1), (5, 1))), ("b6", ((6, 0), (6, 1))), ("b7", ((7, 0),))]
-        last_group = ("b0", ((7, 1),))
+        groups += [("b4", ((4, 0), (5, 0))), ("b5", ((4, 1), (5, 1))), ("b6", ((6, 0),)), ("b7", ((6, 1),))]
+        last_groups = [("b0", ((7, 0),)), ("b1", ((7, 1),))]
         banks = {}
 
         def multiply(group, tables):
             tag, sums = group
-            if sums not in banks:
+            opens = sums not in banks
+            if opens:
                 banks[sums] = psum.tile([P, len(sums) * C], F32, name=f"sums{sums[0][0]}_{sums[0][1]}", tag=tag)
             for n in tables:
                 for u, (e, cb) in enumerate(sums):
+                    opens = opens and n == tables[0]
                     ww, ws = weights(e, n, cb)
                     nc.tensor.matmul_mx(out=banks[sums][:, u * C:(u + 1) * C], lhsT=ww, lhsT_scale=ws,
                                         rhs=gathered("w", n, e * C, (e + 1) * C).bitcast(FP8X4),
                                         rhs_scale=gathered("s", n, e * C, (e + 1) * C),
-                                        start=(n == "q" and u == 0), stop=(n == "k" and u == len(sums) - 1))
+                                        start=(opens and u == 0), stop=(n == "k" and u == len(sums) - 1))
 
         def gate_on_gpsimd(group, offset=None):
             sums = group[1]
@@ -188,21 +189,26 @@ def tile_moe_qkb_kernel(
                 nc.vector.tensor_tensor(dx[cb][:, e * C:(e + 1) * C], banks[sums][:, u * C:(u + 1) * C],
                                         gate_sb[:, e * C:(e + 1) * C], MULT)
 
-        for group in groups:
+        for group in groups[:4] + groups[6:]:
             multiply(group, "q")
         for group in groups[:4]:
             multiply(group, "v")
         for u, group in enumerate(groups[:4]):
             multiply(group, "k")
             gate_on_gpsimd(group, LATE_AT + 9216 + 2048 * u)
-        multiply(last_group, "q")
-        for group in groups[4:] + [last_group]:
-            multiply(group, "v")
+        for group in last_groups:
+            multiply(group, "q")
+        for group in groups[4:6]:
+            multiply(group, "vq")
         for group in groups[4:6]:
             multiply(group, "k")
             gate_on_gpsimd(group)
-        for group in groups[6:] + [last_group]:
+        for group in groups[6:] + last_groups:
+            multiply(group, "v")
+        closing = groups[6:] + last_groups
+        for group in closing:
             multiply(group, "k")
+        for group in closing:
             gate_on_vector(group)
 
         first = [keep.tile([P, T], F32, name=f"first{cb}") for cb in range(2)]

@@ -31,8 +31,9 @@ ROOM_FOR_ALL = 4096
 RAW3_AT = 4096
 LATE_AT = 12288
 
-LEAD = 192
-CUTS = ((LEAD, 608, T), (0, 448, 864, T))
+LEAD = 128
+TAIL = 192
+CUTS = ((2 * LEAD, 704, T), (0, 448, T - TAIL))
 
 
 def tile_moe_qkb_kernel(
@@ -211,17 +212,31 @@ def tile_moe_qkb_kernel(
         for group in closing:
             gate_on_vector(group)
 
-        first = [keep.tile([P, T], F32, name=f"first{cb}") for cb in range(2)]
-        own = keep.tile([P, LEAD], F32, name="own")
+        def columns(pos_sb, cb, lo, hi):
+            return dx[cb][:].indirect(pos_sb[:, lo // PER_COLUMN:hi // PER_COLUMN])
+
+        leads = [(u * LEAD, (u + 1) * LEAD) for u in range(2)]
+        own = [keep.tile([P, LEAD], F32, name=f"own{lo}") for lo, hi in leads]
         opening = keep.tile([P, CUTS[0][1]], F32, name="opening")
-        nc.vector.tensor_copy(own[:], dx[0][:].indirect(pos1_sb[:, 0:LEAD // PER_COLUMN]))
-        nc.vector.tensor_tensor(opening[:, :LEAD], dx[0][:].indirect(pos2_sb[:, 0:LEAD // PER_COLUMN]), own[:], ADD)
+        for u, (lo, hi) in enumerate(leads):
+            nc.vector.tensor_copy(own[u][:], columns(pos1_sb, 0, lo, hi))
+        for u, (lo, hi) in enumerate(leads):
+            nc.vector.tensor_tensor(opening[:, lo:hi], columns(pos2_sb, 0, lo, hi), own[u][:], ADD)
         for cb, cuts in enumerate(CUTS):
+            rows = out[cb * P:(cb + 1) * P]
             for lo, hi in zip(cuts, cuts[1:]):
-                entries = slice(lo // PER_COLUMN, hi // PER_COLUMN)
-                opens = cb == 0 and lo == LEAD
-                both = opening if opens else keep.tile([P, hi - lo], F32, name=f"both{cb}_{lo}")
-                nc.scalar.activation(first[cb][:, lo:hi], dx[cb][:].indirect(pos1_sb[:, entries]), COPY)
-                nc.vector.tensor_tensor(both[:, LEAD:] if opens else both[:], dx[cb][:].indirect(pos2_sb[:, entries]),
-                                        first[cb][:, lo:hi], ADD)
-                nc.sync.dma_start(out[cb * P:(cb + 1) * P, (0 if opens else lo):hi], both[:])
+                first = keep.tile([P, hi - lo], F32, name=f"first{cb}_{lo}")
+                nc.scalar.activation(first[:], columns(pos1_sb, cb, lo, hi), COPY)
+                if lo == 2 * LEAD:
+                    nc.vector.tensor_tensor(opening[:, lo:], columns(pos2_sb, cb, lo, hi), first[:], ADD)
+                    nc.sync.dma_start(rows[:, :hi], opening[:])
+                else:
+                    both = keep.tile([P, hi - lo], F32, name=f"both{cb}_{lo}")
+                    nc.vector.tensor_tensor(both[:], columns(pos2_sb, cb, lo, hi), first[:], ADD)
+                    nc.sync.dma_start(rows[:, lo:hi], both[:])
+        pair = [keep.tile([P, TAIL], F32, name=f"tail{u}") for u in range(2)]
+        closing_sum = keep.tile([P, TAIL], F32, name="closing_sum")
+        for fetched, pos_sb in zip(pair, (pos1_sb, pos2_sb)):
+            nc.scalar.activation(fetched[:], columns(pos_sb, 1, T - TAIL, T), COPY)
+        nc.vector.tensor_tensor(closing_sum[:], pair[0][:], pair[1][:], ADD)
+        nc.sync.dma_start(out[P:, T - TAIL:], closing_sum[:])

from contextlib import ExitStack

import concourse.mybir as mybir

K, T, E, C, N = 256, 1024, 8, 256, 512
FLOPS = 2 * 3 * N * K * E * C

F32 = mybir.dt.float32
BF16 = mybir.dt.bfloat16
I32 = mybir.dt.int32
U32 = mybir.dt.uint32
U16 = mybir.dt.uint16
U8 = mybir.dt.uint8
FP8X4 = mybir.dt.float8_e4m3fn_x4
COPY = mybir.ActivationFunctionType.Copy
MULT = mybir.AluOpType.mult
ADD = mybir.AluOpType.add

P = 128
S = E * C
PAIR = 2 * C
PER_COLUMN = 16
EARLY = E // 2
HALF = EARLY * C
LAST = (E - 2) * C
ROWS_AT = P - 16

ROOM_FOR_HALF = 1376
ROOM_FOR_ALL = 4096

RAW3_AT = 4096
LATE_AT = 12288

LEAD = 128
TAIL = 192
CUTS = ((2 * LEAD, 704, T), (0, 448, T - TAIL))


def tile_moe_qkb_kernel(
    tc, dq_words, dq_scales, dk_words, dk_scales, dv_words, dv_scales,
    wq_words, wq_scales, wk, wv_words, wv_scales, gate, offs, pos1, pos2, out,
):
    nc = tc.nc
    with ExitStack() as ctx:
        keep = ctx.enter_context(tc.tile_pool(name="keep", bufs=1))
        share = ctx.enter_context(tc.tile_pool(name="share", bufs=1))
        psum = ctx.enter_context(tc.psum_pool(name="psum", bufs=1))

        offs_sb = keep.tile([P, S // PER_COLUMN], U16, name="offs_sb")
        pos1_sb = keep.tile([P, T // PER_COLUMN], U16, name="pos1_sb")
        pos2_sb = keep.tile([P, T // PER_COLUMN], U16, name="pos2_sb")
        d_words = {n: keep.tile([P, ROOM_FOR_ALL if n == "q" else ROOM_FOR_HALF], I32, name=f"d{n}_words_sb",
                                align_bytes=64) for n in "qkv"}
        d_scales = {n: keep.tile([P, ROOM_FOR_HALF if n == "k" else ROOM_FOR_ALL], U8, name=f"d{n}_scales_sb",
                                 align_bytes=64) for n in "qkv"}
        w_scales = {n: keep.tile([P, E, K], U8, name=f"w{n}_scales_sb", align_bytes=64) for n in "qv"}
        w_words = {n: keep.tile([P, E, K], I32, name=f"w{n}_words_sb", align_bytes=64) for n in "qv"}
        wk_raw = [share.tile([P, 4, K], F32, name=f"wk_raw{e}", offset=RAW3_AT) if e == EARLY - 1
                  else keep.tile([P, 4, K], F32, name=f"wk_raw{e}") for e in range(EARLY)]
        wk_late = share.tile([P, E - EARLY, 4, K], F32, name="wk_late", offset=LATE_AT)
        gate_sb = keep.tile([P, S], F32, name="gate_sb")
        dx = [keep.tile([P, S], F32, name=f"dx{cb}") for cb in range(2)]

        nc.gpsimd.memset(d_scales["q"][0:ROWS_AT, :T].bitcast(I32), 0)
        for n in "vk":
            nc.vector.memset(d_scales[n][:, :T].bitcast(I32), 0)

        def load_words(n, src):
            nc.sync.dma_start(d_words[n][:, :T], src[0].rearrange("p t d -> p (t d)").bitcast(I32))

        def load_scales(n, src):
            for r in range(4):
                nc.sync.dma_start(d_scales[n][r:P:32, :T].bitcast(I32), src[0].bitcast(I32)[r:16:4, :])

        def load_wk(e):
            nc.sync.dma_start(wk_raw[e][:], wk[e].rearrange("(p j) c -> p j c", j=4))

        def load_weights(n, words, scales):
            nc.sync.dma_start(w_words[n][:], words.rearrange("e s p c d -> p (e s) (c d)").bitcast(I32))
            rows = scales.rearrange("e s b c -> (s b) e c").bitcast(I32)
            for r in range(4):
                nc.sync.dma_start(w_scales[n][r:P:32, :, :].bitcast(I32), rows[r:16:4, :, :])

        nc.sync.dma_start(offs_sb[:], offs)
        nc.sync.dma_start(d_scales["q"][ROWS_AT:, :T].bitcast(I32), dq_scales[0].bitcast(I32))
        load_words("q", dq_words)
        load_wk(0)
        load_scales("v", dv_scales)
        for e in range(1, EARLY):
            load_wk(e)
        load_words("v", dv_words)
        load_words("k", dk_words)
        load_scales("k", dk_scales)
        nc.sync.dma_start(wk_late[:].rearrange("p e j c -> p e (j c)"),
                          wk[EARLY:].rearrange("e (p j) c -> p e (j c)", j=4))
        as_gathered = keep.tile([P, S], U8, name="gqs_rows", align_bytes=64)
        nc.vector.tensor_copy(as_gathered[:], d_scales["q"][:].indirect(offs_sb[:]))
        dealt = keep.tile([P, S], U8, name="gqs_dealt", align_bytes=64)
        for quadrant in range(4):
            row = ROWS_AT + 4 * quadrant
            nc.sync.dma_start(dealt[32 * quadrant:32 * quadrant + 4, :].bitcast(I32),
                              as_gathered[row:row + 4, :].bitcast(I32))
        load_weights("q", wq_words, wq_scales)
        load_weights("v", wv_words, wv_scales)
        nc.sync.dma_start(gate_sb[:], gate)
        nc.sync.dma_start(pos1_sb[:], pos1)
        nc.sync.dma_start(pos2_sb[:], pos2)

        casts = [keep.tile([P, EARLY * K, 4], BF16, name=f"cast{h}", align_bytes=64) for h in range(2)]
        wk_codes = [keep.tile([P, EARLY * K], U32, name=f"wk_codes{h}", align_bytes=64) for h in range(2)]
        wk_scales = [keep.tile([P, EARLY * K], U8, name=f"wk_scales{h}", align_bytes=64) for h in range(2)]
        for e in range(E):
            raw = wk_raw[e][:] if e < EARLY else wk_late[:, e - EARLY]
            at = e % EARLY * K
            nc.scalar.copy(casts[e // EARLY][:, at:at + K], raw.rearrange("p j c -> p c j"))

        def quantise(h):
            nc.vector.quantize_mx(out=wk_codes[h][:].bitcast(FP8X4), scales=wk_scales[h][:],
                                  in_=casts[h][:].rearrange("p c j -> p (c j)"))

        pieces = {}

        def gather(kind, n, lo, hi, offset=None):
            dtype = U32 if kind == "w" else U8
            if offset is None:
                piece = keep.tile([P, hi - lo], dtype, name=f"g{n}{kind}{lo}", align_bytes=64)
            else:
                piece = share.tile([P, hi - lo], dtype, name=f"g{n}{kind}{lo}", align_bytes=64, offset=offset)
            pieces.setdefault((kind, n), []).append((lo, hi, piece))
            table = d_words[n][:].bitcast(U32) if kind == "w" else d_scales[n][:]
            nc.vector.tensor_copy(piece[:], table.indirect(offs_sb[:, lo // PER_COLUMN:hi // PER_COLUMN]))

        def gathered(kind, n, lo, hi):
            return [piece[:, lo - a:hi - a] for a, b, piece in pieces[kind, n] if a <= lo and hi <= b][0]

        def weights(e, n, cb):
            lo, hi = cb * P, (cb + 1) * P
            if n != "k":
                return w_words[n][:, e, lo:hi].bitcast(FP8X4), w_scales[n][:, e, lo:hi]
            h, at = e // EARLY, e % EARLY * K
            return wk_codes[h][:, at + lo:at + hi].bitcast(FP8X4), wk_scales[h][:, at + lo:at + hi]

        pieces["s", "q"] = [(0, S, dealt)]
        gather("w", "q", 0, S)
        gather("s", "v", 0, S)
        quantise(0)
        gather("w", "v", 0, HALF, RAW3_AT + 64 - 4 * HALF)
        gather("w", "k", 0, HALF, RAW3_AT + 64 + HALF)
        gather("s", "k", 0, HALF, RAW3_AT + 64)
        quantise(1)
        gather("w", "v", HALF, S, LATE_AT)
        gather("w", "k", HALF, LAST, LATE_AT + 4096)
        gather("s", "k", HALF, LAST, LATE_AT + 8192)
        gather("w", "k", LAST, S, LATE_AT + 6144)
        gather("s", "k", LAST, LAST + C, LATE_AT + 8192 + PAIR)
        gather("s", "k", LAST + C, S, LATE_AT + 8192 + PAIR + C)

        groups = [(f"b{2 * cb + pair}", ((2 * pair, cb), (2 * pair + 1, cb))) for cb in range(2) for pair in range(2)]
        groups += [("b4", ((4, 0), (5, 0))), ("b5", ((4, 1), (5, 1))), ("b6", ((6, 0),)), ("b7", ((6, 1),))]
        last_groups = [("b0", ((7, 0),)), ("b1", ((7, 1),))]
        banks = {}

        def multiply(group, tables):
            tag, sums = group
            opens = sums not in banks
            if opens:
                banks[sums] = psum.tile([P, len(sums) * C], F32, name=f"sums{sums[0][0]}_{sums[0][1]}", tag=tag)
            for n in tables:
                for u, (e, cb) in enumerate(sums):
                    opens = opens and n == tables[0]
                    ww, ws = weights(e, n, cb)
                    nc.tensor.matmul_mx(out=banks[sums][:, u * C:(u + 1) * C], lhsT=ww, lhsT_scale=ws,
                                        rhs=gathered("w", n, e * C, (e + 1) * C).bitcast(FP8X4),
                                        rhs_scale=gathered("s", n, e * C, (e + 1) * C),
                                        start=(opens and u == 0), stop=(n == "k" and u == len(sums) - 1))

        def gate_on_gpsimd(group, offset=None):
            sums = group[1]
            e, cb = sums[0]
            if offset is None:
                plain = keep.tile([P, PAIR], F32, name=f"plain{e}_{cb}")
            else:
                plain = share.tile([P, PAIR], F32, name=f"plain{e}_{cb}", offset=offset)
            nc.scalar.copy(plain[:], banks[sums][:])
            nc.gpsimd.tensor_tensor(dx[cb][:, e * C:e * C + PAIR], plain[:], gate_sb[:, e * C:e * C + PAIR], MULT)

        def gate_on_vector(group):
            sums = group[1]
            for u, (e, cb) in enumerate(sums):
                nc.vector.tensor_tensor(dx[cb][:, e * C:(e + 1) * C], banks[sums][:, u * C:(u + 1) * C],
                                        gate_sb[:, e * C:(e + 1) * C], MULT)

        for group in groups[:4] + groups[6:]:
            multiply(group, "q")
        for group in groups[:4]:
            multiply(group, "v")
        for u, group in enumerate(groups[:4]):
            multiply(group, "k")
            gate_on_gpsimd(group, LATE_AT + 9216 + 2048 * u)
        for group in last_groups:
            multiply(group, "q")
        for group in groups[4:6]:
            multiply(group, "vq")
        for group in groups[4:6]:
            multiply(group, "k")
            gate_on_gpsimd(group)
        for group in groups[6:] + last_groups:
            multiply(group, "v")
        closing = groups[6:] + last_groups
        for group in closing:
            multiply(group, "k")
        for group in closing:
            gate_on_vector(group)

        def columns(pos_sb, cb, lo, hi):
            return dx[cb][:].indirect(pos_sb[:, lo // PER_COLUMN:hi // PER_COLUMN])

        leads = [(u * LEAD, (u + 1) * LEAD) for u in range(2)]
        own = [keep.tile([P, LEAD], F32, name=f"own{lo}") for lo, hi in leads]
        opening = keep.tile([P, CUTS[0][1]], F32, name="opening")
        for u, (lo, hi) in enumerate(leads):
            nc.vector.tensor_copy(own[u][:], columns(pos1_sb, 0, lo, hi))
        for u, (lo, hi) in enumerate(leads):
            nc.vector.tensor_tensor(opening[:, lo:hi], columns(pos2_sb, 0, lo, hi), own[u][:], ADD)
        for cb, cuts in enumerate(CUTS):
            rows = out[cb * P:(cb + 1) * P]
            for lo, hi in zip(cuts, cuts[1:]):
                first = keep.tile([P, hi - lo], F32, name=f"first{cb}_{lo}")
                nc.scalar.activation(first[:], columns(pos1_sb, cb, lo, hi), COPY)
                if lo == 2 * LEAD:
                    nc.vector.tensor_tensor(opening[:, lo:], columns(pos2_sb, cb, lo, hi), first[:], ADD)
                    nc.sync.dma_start(rows[:, :hi], opening[:])
                else:
                    both = keep.tile([P, hi - lo], F32, name=f"both{cb}_{lo}")
                    nc.vector.tensor_tensor(both[:], columns(pos2_sb, cb, lo, hi), first[:], ADD)
                    nc.sync.dma_start(rows[:, lo:hi], both[:])
        pair = [keep.tile([P, TAIL], F32, name=f"tail{u}") for u in range(2)]
        closing_sum = keep.tile([P, TAIL], F32, name="closing_sum")
        for fetched, pos_sb in zip(pair, (pos1_sb, pos2_sb)):
            nc.scalar.activation(fetched[:], columns(pos_sb, 1, T - TAIL, T), COPY)
        nc.vector.tensor_tensor(closing_sum[:], pair[0][:], pair[1][:], ADD)
        nc.sync.dma_start(out[P:, T - TAIL:], closing_sum[:])
